import numpy as np, ml_dtypes
CORES = [2,6,10,14,18,22,26,30]
N = 8
BF = ml_dtypes.bfloat16
def gentries(a):
    return np.ascontiguousarray(a.reshape(8, 16, -1).transpose(0, 2, 1)).reshape(8, -1)
def gtable(e):
    e = np.asarray(e); return np.ascontiguousarray(e.reshape(8, -1, 16).transpose(0, 2, 1)).reshape(128, -1).astype(np.int32)
V, G, CAP, D, P, RO = 1024, 256, 64, 8, 2048, 4
W = V + (N - 1) * G
def paths(rng, n):
    s = (N, 8, 16, V)
    q = np.where(rng.random(s) < 0.6, np.arange(N).reshape(N, 1, 1, 1), rng.integers(0, N, s))
    u = np.where(rng.random(s) < 0.6, (np.arange(V) + rng.integers(-8, 9, s)) % V, rng.integers(0, V, s))
    a = q * V + u + 1; a[:, :, 0] = (np.arange(N * V) + 1).reshape(N, 1, V)
    return np.where(np.arange(16).reshape(16, 1) < n, a, 0)
def parts(rng):
    s = (N, 8, D, V)
    n = np.where(rng.random((N, 8, 1, V)) < rng.choice(np.array([0.1, 0.3, 0.6]), (N, 8, 1, 1)), 0, rng.integers(1, 17, (N, 8, 1, V)))
    return {"path": paths(rng, n), "toll": rng.integers(0, 256, (N, 128, W)),
            "nb": np.where(rng.random(s) < 0.5, (np.arange(V) + rng.integers(-8, 9, s)) % V, rng.integers(0, W, s)),
            "pr": rng.integers(0, 16, s) % rng.choice(np.array([2, 4, 16]), (N, 8, 1, 1)),
            "dn": np.where(rng.random(s) < 0.75, 15, rng.integers(0, RO + 1, s)),
            "org": rng.random((N, 8, V)) < rng.choice(np.array([0.01, 0.05]), (N, 8, 1)),
            "shown": np.ascontiguousarray(np.argsort(rng.random((N, 8, N - 1, V)), axis=-1)[..., :G]),
            "at": rng.integers(0, W, (N, 8, P))}
def pack(d):
    return {"path0": np.ascontiguousarray(d["path"].reshape(N, 128, V)).astype(np.int32), "toll": d["toll"].astype(np.float32).astype(BF),
            "nb": np.stack([gtable(a.reshape(8, -1)) for a in d["nb"]]), "lk": (16 * d["dn"] + d["pr"]).reshape(N, 8, D * V).astype(np.int32),
            "org": d["org"].astype(np.int32), "shown": np.stack([gtable(a.reshape(8, -1)) for a in d["shown"]]), "at0": np.stack([gtable(a) for a in d["at"]])}
def setup_inputs(rng):
    return pack(parts(rng))
def late(rng, d, p, q, g):
    odd = 2 * rng.permutation(V // 2) + 1; even = 2 * rng.permutation(V // 2); u = V // 16
    x, y1, y3, f0, f1 = odd[:u], odd[u:2 * u], odd[2 * u:3 * u], odd[3 * u:3 * u + 16], odd[3 * u + 16:3 * u + 32]
    z0, z2 = even[:u], even[u:2 * u]
    quiet = np.concatenate([even[2 * u:3 * u], odd[3 * u + 32:4 * u + 32]]); rd = np.concatenate([even[3 * u:], odd[4 * u + 32:]])
    for k in (y1, y3, f1, z2, quiet): p[:, k] = 0
    p[8:, f0] = 0; p[1:, f0[:8]] = 0
    o = d["org"][q, g]; o[:] = False; o[f0] = True; o[f1] = True
    nb = d["nb"][q, g]; dn = d["dn"][q, g]
    for k, f, m in ((x, f0, (2, 15)), (y1, f0, (3, 15)), (y3, f1, (4, 15)), (z0, f0[:8], (15, 15)), (z2, f1, (3, 15)), (quiet, f0, (0, 0))):
        nb[:, k] = rng.choice(f, len(k)); dn[:, k] = rng.choice(np.array(m), len(k))
    nb[:, rd] = np.where(rng.random((D, len(rd))) < 0.75, rng.integers(V, W, (D, len(rd))), nb[:, rd])
    for e in range(N - 1):
        sc = (q + e + g // 2) % 4; m = CAP - 1 + (q + e) % 3; n = rng.integers(0, 4, 5)
        if sc == 0: n[0] = rng.integers(8, 20); n[1] = rng.integers(3, 7); n[2] = 0; n[3] = rng.integers(0, 2)
        if sc == 1: n[2] = m - n[1]
        if sc == 2: n[3] = m
        if sc == 3: n[1:3] = 0; n[4] = m
        a = np.concatenate([rng.choice(k, int(i)) for k, i in zip((z0, x, y1, z2, y3), n)])
        if sc > 0: a = rng.permutation(a)
        a = np.concatenate([rng.choice(quiet, G - len(a)), a])
        if sc > 0 and rng.random() < 0.5: a = rng.permutation(a)
        d["shown"][q, g, e] = a
def setup_inputs_room(rng):
    d = parts(rng); path = paths(rng, rng.integers(1, 17, (N, 8, 1, V))); odd = 2 * np.arange(V // 2) + 1; h = V // 4
    for q in range(N):
        for g in range(0, 8, 2):
            o = rng.permutation(odd); a, b = o[:h], o[h:]
            path[q, g][:, b] = 0
            for e in range(N - 1):
                n = int(rng.choice(np.array([0, 1, CAP - 1, CAP, CAP + 1, G])))
                if q < 2 and e == 0: n = ((CAP, CAP + 1, G, CAP - 1), (1, 0, CAP, CAP + 1))[q][g // 2]
                d["shown"][q, g, e] = rng.permutation(np.concatenate([rng.permutation(a)[:n], rng.permutation(b)[:G - n]]))
        for g in range(1, 8, 2): late(rng, d, path[q, g], q, g)
    d["path"] = path
    return pack(d)
def setup_inputs_ties(rng):
    d = parts(rng); s = (N, 8, D, V)
    path = paths(rng, rng.choice(np.array([1, 14, 15, 16]), (N, 8, 1, V)))
    d["pr"] = rng.choice(np.array([0, 7, 14]), (N, 8, 1, 1)) + rng.integers(0, 2, s) * rng.integers(0, 2, (N, 8, 1, 1))
    d["dn"] = rng.choice(np.array([0, 1, 2, RO - 1, RO, 15, 15, 15]), s)
    v = np.arange(1, V, 4); c = v + 2; j = np.arange(16).reshape(16, 1); z = len(v); x = np.arange(z); m = N * V // 2
    wt = np.array([1, 37, 101, 13, 89, 53, 127, 7, 71, 113, 29, 97, 61, 19, 109, 43])
    for q in range(N):
        for g in (1, 3, 5, 7):
            lo, hi = {1: (2, 15), 3: (2, 16), 5: (3, 15), 7: (8, 15)}[g]
            n = rng.integers(lo, hi, z); kd = rng.integers(0, 6, z); rim = 128 if g == 7 else 0
            if g == 3: n = np.where(kd == 5, 15, np.where(kd == 4, np.minimum(n, 14), n))
            a = 2 * rng.integers(rim, m - rim, (16, z)) + 1; a[0] = q * V + c + 1; a = np.where(j < n, a, 0)
            h = np.flatnonzero((kd == 4) & (x % 2 == 0))
            if g == 3: a[n[h] - 1, h] = N * V
            b = np.concatenate([a[:1], a[:15]])
            if g == 1:
                b = np.take_along_axis(a, np.clip(n - j, 0, 15), 0); b = np.where((j >= 1) & (j <= n), b, 0)
            elif g == 5:
                i = rng.integers(2, n); k = rng.integers(i + 1, n + 1)
                b[i, x] = a[k - 1, x]; b[k, x] = a[i - 1, x]
            elif g == 3:
                k = np.where(kd == 5, 15, rng.integers(1, n + 1))
                by = np.where(kd == 1, V * rng.integers(1, N, z), np.where(kd == 2, 2, np.where(kd == 3, 2 ** rng.integers(1, 13, z), 2 * rng.integers(1, m, z))))
                b[k, x] = np.where(kd == 4, b[k, x], (b[k, x] - 1 + by) % (N * V) + 1)
                b[n[h], h] = 0
                h = np.flatnonzero((kd == 4) & (x % 2 == 1)); b[n[h] + 1, h] = N * V
                h = np.flatnonzero(kd == 5)[::3]; b[15, h] = 0
            else:
                kd = kd % 3; o = np.argsort(np.where((j >= 2) & (j <= n), rng.random((16, z)), 2.0), axis=0)[:4]
                by = np.where(kd == 0, np.array([[2], [2], [-2], [-2]]), 0); w2 = 2 ** rng.integers(1, 7, (2, z))
                by[0] = np.where(kd == 1, w2[0], np.where(kd == 2, 2 * wt[o[1]], by[0]))
                by[1] = np.where(kd == 1, -w2[1], np.where(kd == 2, -2 * wt[o[0]], by[1]))
                b[o, x] = b[o, x] + by
            b[0] = q * V + v + 1
            path[q, g][:, c] = a; path[q, g][:, v] = b
            d["nb"][q, g][:, v] = c; d["dn"][q, g][:, v] = 15; d["org"][q, g, v] = False
            for e in range(N - 1): d["shown"][q, g, e] = rng.permutation(v)[:G]
    d["path"] = path
    return pack(d)
def setup_inputs_loops(rng):
    d = parts(rng); nb = d["nb"]; snd = d["shown"]
    for g in range(8): nb[N - 1, g, :, V - 1] = 2 * rng.permutation(V // 2 - 1)[:D] + 1
    d["dn"][N - 1, :, :, V - 1] = 15; d["org"][N - 1, :, V - 1] = False
    n = np.where(rng.random((N, 8, 1, V)) < 0.8, 15, rng.integers(1, 16, (N, 8, 1, V))); path = paths(rng, n)
    for q in range(N):
        for g in range(8):
            for i in range(D):
                v = np.flatnonzero((nb[q, g, i] < V) & (rng.random(V) < 0.3)); u = nb[q, g, i][v]
                who = np.where(rng.random(len(v)) < 0.7, q, (q + 1) % N)
                path[q, g][(rng.random(len(v)) * n[q, g, 0, u]).astype(np.int64), u] = who * V + v + 1
                for e in range(N - 1):
                    b = (q + e + 1) % N; k = nb[b, g, i] - V - e * G
                    v = np.flatnonzero((k >= 0) & (k < G) & (rng.random(V) < 0.5)); u = snd[q, g, e][k[v]]
                    path[q, g][(rng.random(len(v)) * n[q, g, 0, u]).astype(np.int64), u] = b * V + v + 1
    for g in range(8):
        u = nb[N - 1, g, :, V - 1]; path[N - 1, g][(rng.random(D) * n[N - 1, g, 0, u]).astype(np.int64), u] = N * V
    d["path"] = path
    return pack(d)
def setup_inputs_ends(rng):
    d = parts(rng); nb = d["nb"]
    d["shown"][:, ::2] = rng.choice(np.array([0, V - 1, V // 2, 3]), (N, 4, N - 1, G)); d["at"][:, ::2] = rng.choice(np.array([0, V - 1, V, W - 1]), (N, 4, P))
    nb[:, 0] = nb[:, 0, :1]; nb[:, 2] = rng.integers(V, W, (N, D, V)); nb[:, 4] = rng.integers(0, V, (N, D, V))
    nb[:, 6] = rng.choice(np.array([0, V - 1, V, W - 1]), (N, D, V))
    d["path"][:, 3] = 0; d["org"][:, 3] = False
    d["path"][:, 1] = 0; d["org"][:, 1] = False; d["org"][0, 1, V - 1] = True
    d["org"][:, 5] = True; d["dn"][:, 7] = 0; d["toll"][:, :, ::3] = 255
    return pack(d)
def setup_inputs_spread(rng):
    d = parts(rng); s = (N, 8, D, V)
    n = np.minimum(np.exp2(4.2 * rng.random((N, 8, 1, V))).astype(np.int64) - 1, 16)
    a = np.minimum(np.exp2(13 * rng.random((N, 8, 16, V))).astype(np.int64), N * V)
    d["path"] = np.where(np.arange(16).reshape(16, 1) < n, a, 0)
    d["nb"] = rng.integers(0, W, s); d["pr"] = rng.integers(0, 16, s); d["dn"] = rng.integers(0, 16, s)
    d["org"] = rng.random((N, 8, V)) < np.exp2(-8 * rng.random((N, 8, 1))); d["shown"] = rng.integers(0, V, (N, 8, N - 1, G))
    d["toll"] = np.minimum((np.exp2(8 * rng.random((N, 1, W))) * rng.random((N, 128, W))).astype(np.int64), 255)
    d["at"] = np.minimum((W * rng.random((N, 8, P)) ** 3).astype(np.int64), W - 1)
    return pack(d)
def check_inputs(d):
    bad = []
    for k, hi in (("path0", N * V), ("nb", W - 1), ("lk", 255), ("org", 1), ("shown", V - 1), ("at0", W - 1)):
        if np.min(d[k]) < 0 or np.max(d[k]) > hi: bad.append("range of " + k)
    t = d["toll"].astype(np.float32)
    if not np.all((t >= 0) & (t <= 255) & (t == np.floor(t))): bad.append("toll: whole numbers from 0 to 255")
    p = d["path0"].reshape(-1, 16, V)
    if np.any((p[:, :15] == 0) & (p[:, 1:] != 0)): bad.append("filled rows of path0 come first")
    return bad
def reference(path0, toll, nb, lk, org, shown, at0):
    A = np.zeros((N, 8, 16, W), np.int32); A[..., :V] = path0.reshape(N, 8, 16, V)
    nbl = np.stack([gentries(a) for a in nb]).astype(np.int64).reshape(N, 8, D, V)
    sl = np.stack([gentries(a) for a in shown]).astype(np.int64).reshape(N, 8, N - 1, G)
    pos = [gentries(a).astype(np.int64) for a in at0]
    pr = (lk & 15).reshape(N, 8, D, V); dn = (lk >> 4).reshape(N, 8, D, V)
    fee = toll.astype(np.float32).astype(np.int32).reshape(N, 8, 16, W); S = np.zeros((N, 8, 16, P), np.int32)
    me = np.arange(V, dtype=np.int64); rest = np.broadcast_to(np.arange(V, W, dtype=np.int64), (8, W - V))
    for t in range(RO):
        for r in range(N):
            name = (r * V + me + 1).astype(np.int32)
            c = np.take_along_axis(A[r], nbl[r].reshape(8, 1, D * V), 2).reshape(8, 16, D, V)
            length = np.add.reduce((c > 0).astype(np.int32), axis=1)
            ok = (t < dn[r]) & (c[:, 0] > 0) & (c[:, 15] == 0) & ~np.any(c == name, axis=1)
            w = np.argmax(np.where(ok, 32 * pr[r] + 16 - length, -1), axis=1)
            some = np.any(ok, axis=1) & (org[r] == 0)
            best = np.take_along_axis(c, w[:, None, None, :], 2)[:, :, 0]
            new = np.zeros((8, 16, V), np.int32)
            new[:, 0] = np.where(some | (org[r] == 1), name, 0); new[:, 1:] = np.where(some[:, None], best[:, :15], 0)
            nh = np.where(some, np.take_along_axis(nbl[r], w[:, None], 1)[:, 0], me)
            A[r, :, :, (t & 1):V:2] = new[:, :, (t & 1)::2]
            pos[r] = np.take_along_axis(np.concatenate([nh, rest], axis=1), pos[r], 1)
            S[r] = (S[r] + np.take_along_axis(fee[r], pos[r][:, None], 2)) & 255
        for q in range(N):
            for d in range(1, N):
                b = (q + d) % N; lo = V + (d - 1) * G
                cur = np.take_along_axis(A[q], sl[q, :, d - 1][:, None], 2); old = A[b, :, :, lo:lo + G].copy()
                ch = np.any(cur != old, axis=1).astype(np.int64); before = np.add.accumulate(ch, axis=1) - ch
                A[b, :, :, lo:lo + G] = np.where(((ch == 1) & (before < CAP))[:, None], cur, old)
    return {"ypath": A[..., :V].reshape(N, 128, V).astype(np.float32), "ysum": S.reshape(N, 128, P).astype(np.float32).astype(BF)}

@@ -1,0 +1,663 @@
+from concourse.bass import DstId, RemoteDMATransfer
+from concourse.mybir import AluOpType as ALU, ActivationFunctionType as ACT
+
+N, V, G, W, P, RO = 8, 1024, 256, 2816, 2048, 4
+GH = W - V
+BIG = float(1 << 24)
+PRE = (0, 8, GH, GH, 0)
+F32, BF, I32, U16 = "float32", "bfloat16", "int32", "uint16"
+
+
+def _sb(n, dt):
+    return ("sbuf", [128, n], dt)
+
+
+SCRATCH = {
+    "B0": _sb(V + 8, F32), "B1": _sb(8 + W + 8, F32), "B2": _sb(GH + W + 8, F32), "B3": _sb(GH + W + 8, F32),
+    "B4": _sb(V, F32), "SND": _sb(GH, F32),
+    "pathi": _sb(V, I32), "nbi": _sb(512, I32), "nbf": _sb(512, F32),
+    "X": ("sbuf", [128, 8, 2, 32], I32), "O": ("sbuf", [128, 8, 2, 32], I32),
+    "Xb": _sb(512, BF), "DNb": _sb(512, BF), "Ob": _sb(512, BF),
+    "shi": _sb(112, I32), "shu": _sb(112, U16), "SA0": _sb(112, F32), "SA1": _sb(112, F32), "slot": _sb(112, F32),
+    "ati": _sb(128, I32), "atu": _sb(128, U16),
+    "kci": _sb(4, I32), "gqi": _sb(4, I32), "col": _sb(16, F32),
+    "SV": _sb(128, F32), "RG": _sb(128, F32), "DD": _sb(128, F32), "RQ": _sb(128, F32),
+    "SHF": _sb(512, F32), "IDb": _sb(128, BF), "IDf": _sb(128, F32), "NEG": _sb(128, BF), "I20": _sb(128, BF),
+    "DK": _sb(128, BF), "ONE": _sb(128, BF), "R16": _sb(128, BF), "I192": _sb(128, BF),
+    "MEQ": _sb(144, BF), "MSG": _sb(144, BF), "MPK": _sb(144, F32), "SHT": _sb(128, F32),
+    "BOS": _sb(128, BF), "TMS": _sb(128, BF), "C191": _sb(112, BF), "RST": _sb(112, BF),
+    "NM0": _sb(V, F32), "NM1": _sb(V, F32), "TT0": _sb(512, F32), "TT1": _sb(512, F32), "ZT": _sb(8, F32),
+    "L0": _sb(512, U16), "L": _sb(512, U16), "CST": _sb(512, F32), "LK": _sb(512, BF),
+    "DT0": _sb(512, BF), "DT1": _sb(512, BF), "DT2": _sb(512, BF), "DT3": _sb(512, BF),
+    "DP0": _sb(64, F32), "DP": _sb(128, F32), "DN": _sb(128, F32), "DN8": _sb(64, F32),
+    "EQ": _sb(4096, BF), "SG": _sb(4096, BF), "RUN": _sb(512, F32),
+    "RI": _sb(64, I32), "RA": _sb(64, I32), "NI": _sb(32, I32), "NA": _sb(32, I32), "PL": _sb(128, U16), "NH": _sb(256, U16),
+    "PG": _sb(512, F32),
+    "NE": _sb(GH, BF), "CH": _sb(112, BF), "SC": _sb(112, BF), "M1": _sb(112, F32), "M2": _sb(112, F32), "XI": _sb(112, U16),
+    "TP": _sb(W, F32), "H": _sb(W, F32), "A": _sb(V, F32), "X1": _sb(V, F32), "X2": _sb(V, F32),
+    "QI": _sb(64, I32), "QA": _sb(64, I32), "Q1": _sb(64, U16), "Q2": _sb(64, U16),
+    "tg": _sb(GH, BF), "FL": _sb(GH, BF), "I4": _sb(128, BF), "I256": _sb(128, BF), "FW": _sb(W, BF),
+    "ZI": _sb(V, I32), "ZA": _sb(V, I32), "YS": _sb(P, BF),
+}
+for _b in range(8):
+    SCRATCH["ps%d" % _b] = ("psum", [128, 512], F32)
+
+SEMAPHORES = ["qV", "qS", "qP", "qG", "sent", "arr0", "arr1", "arr2"] + ["d%d" % _b for _b in range(32)]
+
+
+def add_op(pl, q, fn, reads, writes, sem=None, inc=16):
+    pl["ops"].append({"q": q, "fn": fn, "r": reads, "w": writes, "sem": sem, "inc": inc})
+
+
+def overlap(a, b):
+    return a[1].startswith("ps") or (a[2] < b[3] and b[2] < a[3])
+
+
+def emit(pl, g, T):
+    ops = pl["ops"]
+    queues = {"V": g.vector, "S": g.scalar, "P": g.tensor, "G": g, "Y": g.sync}
+    total = {}
+    for o in ops:
+        if o["sem"] is not None:
+            total[o["sem"]] = total.get(o["sem"], 0) + o["inc"]
+    known = {q: {} for q in queues}
+    touch = {}
+    for n, o in enumerate(ops):
+        q = o["q"]
+        o["key"] = o["sem"] if o["sem"] is not None else "q" + q
+        accs = [(a, False) for a in o["r"]] + [(a, True) for a in o["w"]]
+        deps = set()
+        for acc, wr in accs:
+            for (m, b, bw) in touch.get(acc[1], []):
+                e = ops[m]
+                if overlap(acc, b) and not (q == "P" and e["q"] == "P") and (wr or bw or (acc[1].startswith("ps") and e["q"] != q)):
+                    deps.add(m)
+        for acc, wr in accs:
+            touch.setdefault(acc[1], []).append((n, acc, wr))
+        o["waits"] = []
+        if q == "X":
+            o["vc"] = {o["key"]: len(ops)}
+            continue
+        kn = known[q]
+        for m in sorted(deps, reverse=True):
+            e = ops[m]
+            if (e["sem"] is not None and e["sem"] == o["sem"]) or kn.get(e["key"], -1) >= m:
+                continue
+            o["waits"].append(m)
+            e["need"] = True
+            for x in ([e] if e["sem"] is None else [x for x in ops[:n] if x["sem"] == e["sem"]]):
+                for k, val in x["vc"].items():
+                    if kn.get(k, -1) < val:
+                        kn[k] = val
+        o["vc"] = dict(kn)
+        o["vc"][o["key"]] = len(ops) if o["sem"] is not None else n
+    count = {}
+    for o in ops:
+        if o["sem"] is None and o.get("need"):
+            count[o["key"]] = count.get(o["key"], 0) + 1
+            o["val"] = count[o["key"]]
+    waited = set()
+    for o in ops:
+        if o["q"] == "X":
+            continue
+        h = queues[o["q"]]
+        for m in o["waits"]:
+            e = ops[m]
+            if e["sem"] is None:
+                h.wait_ge(T.sem[e["key"]], e["val"])
+            else:
+                h.wait_ge(T.sem[e["sem"]], total[e["sem"]])
+                waited.add(e["sem"])
+        ins = o["fn"](h)
+        if o["sem"] is not None:
+            if o["sem"] != "sent":
+                ins.then_inc(T.sem[o["sem"]], o["inc"])
+        elif o.get("need"):
+            ins.then_inc(T.sem[o["key"]], 1)
+    for s in total:
+        if s not in waited:
+            g.wait_ge(T.sem[s], total[s])
+
+
+def rank_program(g, core, T, topo):
+    r = T.rank_of(core)
+    if r is None:
+        return
+    pl = {"ops": [], "dma": {}, "ndma": [0]}
+
+    def R(name, lo=0, hi=None, step=1, p1=128):
+        t = T[name]
+        if hi is None:
+            hi = t.shape[1]
+        return (t[0:p1, lo:hi] if step == 1 else t[0:p1, lo:hi:step], name, lo, hi)
+
+    def R4(name, e, rows=128):
+        return (T[name][0:rows, :, e, :], name, 0, 512)
+
+    def IND(win, off):
+        return (win[0].indirect(off[0]), win[1], win[2], win[3], off)
+
+    def rd(*aps):
+        out = []
+        for a in aps:
+            if isinstance(a, tuple):
+                out.append(a)
+                if len(a) == 5:
+                    out.append(a[4])
+        return out
+
+    def val(a):
+        return a[0] if isinstance(a, tuple) else a
+
+    def copy(out, in_):
+        add_op(pl, "V", lambda h: h.tensor_copy(out[0], in_[0]), rd(in_), [out])
+
+    def tt(out, a, b, op):
+        add_op(pl, "V", lambda h: h.tensor_tensor(out[0], a[0], b[0], op), rd(a, b), [out])
+
+    def ts(out, a, s1, op0, s2=None, op1=None):
+        if op1 is None:
+            add_op(pl, "V", lambda h: h.tensor_scalar(out[0], a[0], val(s1), None, op0), rd(a, s1), [out])
+        else:
+            add_op(pl, "V", lambda h: h.tensor_scalar(out[0], a[0], val(s1), val(s2), op0, op1), rd(a, s1, s2), [out])
+
+    def memset(out, c):
+        add_op(pl, "V", lambda h: h.memset(out[0], c), [], [out])
+
+    def act(out, a, func=ACT.Identity, scale=None, bias=None):
+        kw = {}
+        if scale is not None:
+            kw["scale"] = val(scale)
+        if bias is not None:
+            kw["bias"] = val(bias)
+        add_op(pl, "S", lambda h: h.activation(out[0], a[0], func, **kw), rd(a, scale, bias), [out])
+
+    def move(out, in_, on_v):
+        if on_v:
+            copy(out, in_)
+        else:
+            act(out, in_)
+
+    def mm(out, lhsT, rhs, start, stop):
+        add_op(pl, "P", lambda h: h.matmul(out[0], lhsT[0], rhs[0], start, stop), [lhsT, rhs], [out])
+
+    def iota(out, pattern, base, cm, flt=True):
+        if flt:
+            add_op(pl, "G", lambda h: h.iota(out[0], pattern, base, cm, allow_small_or_imprecise_dtypes=True), [], [out])
+        else:
+            add_op(pl, "G", lambda h: h.iota(out[0], pattern, base, cm), [], [out])
+
+    def select(out, in_, op, fill):
+        add_op(pl, "G", lambda h: h.affine_select(out[0], in_[0], [[-1, 128]], op, fill, 0, 1), [in_], [out])
+
+    def dma(q, out, in_, grp=None, add=False):
+        if grp not in pl["dma"]:
+            s = "d%d" % pl["ndma"][0]
+            pl["ndma"][0] += 1
+            if grp is not None:
+                pl["dma"][grp] = s
+        else:
+            s = pl["dma"][grp]
+        if add:
+            add_op(pl, q, lambda h: h.dma_start(val(out), val(in_), accum_op=ALU.add), rd(in_, out), rd(out), sem=s)
+        else:
+            add_op(pl, q, lambda h: h.dma_start(val(out), val(in_)), rd(in_), rd(out), sem=s)
+
+    here = topo.chip(core)
+    dest = {d: T.cores[(r + d) % N] for d in range(1, N)}
+    near = [d for d in dest if topo.chip(dest[d]) == here]
+    mate = [d for d in dest if topo.mates(here, topo.chip(dest[d]))]
+    plane = [d for d in dest if topo.same_plane(here, topo.chip(dest[d]))]
+    both = [d for d in dest if d not in near + mate + plane]
+    chunks = [both, [plane[0], mate[0]], [plane[1], mate[1]] + near]
+    order = [d for ch in chunks for d in ch]
+    far_engines = topo.engines(core, dest[both[0]])
+    share = len(far_engines) // 2
+
+    dma("Y", R("nbi"), T.nb[:])
+    dma("S", R("pathi", 0, 512), T.path0[:, 0:512])
+    dma("S", R("pathi", 512, V), T.path0[:, 512:V])
+    for k in range(8):
+        dma("Y", (T.X[:, k], "X", 0, 512), T.lk[k], grp="lk")
+    for k in range(8):
+        dma("Y", (T.O[0:16, k], "O", 0, 512), T.org[k], grp="org")
+    for k, d in enumerate(order):
+        dma("Y", R("shi", 16 * k, 16 * k + 16), T.shown[:, 16 * d - 16:16 * d], grp="shown")
+    dma("Y", R("ati"), T.at0[:])
+
+    iota(R("SV"), [[-16, 8], [256, 2], [-2, 8]], 0, 1)
+    iota(R("kci", 0, 1), [[0, 1]], 0, 1, flt=False)
+    iota(R("DD"), [[-1, 128]], 0, 1)
+    iota(R("RG"), [[1, 8], [0, 16]], 0, 0)
+    iota(R("NM0"), [[0, 2], [2, 512]], r * V + 1, 0)
+    iota(R("RQ"), [[0, 8], [1, 16]], 0, 0)
+
+    GC, QC, WA, WB, WC, KC, Q0, QN, C2, Q2 = [R("col", j, j + 1) for j in range(10)]
+    for n in ("MEQ", "MSG", "ZT", "DP0", "DP", "DN", "MPK"):
+        memset(R(n), 0.0)
+    for k in range(4):
+        ts(R("SHF", 128 * k, 128 * k + 128), R("SV"), 256.0 * (k & 1) + (k >> 1), ALU.is_equal)
+    ts(R("gqi", 0, 1), R("kci", 0, 1), 4, ALU.arith_shift_right)
+    ts(R("gqi", 1, 2), R("kci", 0, 1), 15, ALU.bitwise_and)
+    memset(R("ONE"), 1.0)
+    copy(R("col", 0, 2), R("gqi", 0, 2))
+    ts(R("IDb"), R("DD"), 0.0, ALU.is_equal)
+    ts(WA, QC, 0.0, ALU.is_equal, BIG + 32768.0, ALU.mult)
+    ts(WB, QC, 15.0, ALU.is_equal, 32768.0 - BIG, ALU.mult)
+    ts(KC, GC, -4096.0, ALU.mult, 4096.0 * 127, ALU.add)
+    ts(Q0, QC, 0.0, ALU.is_equal)
+    ts(R("ZT", 1, 2), QC, 15.0, ALU.is_equal)
+    ts(R("BOS"), R("RG"), GC, ALU.is_equal, -8192.0, ALU.mult)
+    ts(WC, WA, WB, ALU.add, -32768.0, ALU.add)
+    ts(R("MEQ", 15, 143, 16), R("RG", 0, 128, 16), GC, ALU.is_equal, -BIG, ALU.mult)
+    copy(R("B0", V, V + 8), R("ZT"))
+    ts(R("MSG", 15, 143, 16), R("RG", 0, 128, 16), GC, ALU.is_equal, WC, ALU.mult)
+    copy(R("nbf"), R("nbi"))
+    for n, c in (("I20", float(1 << 20)), ("NEG", -BIG), ("I192", 192 * BIG), ("IDf", 1.0), ("DK", KC), ("I4", 4.0), ("I256", -256.0)):
+        act(R(n), R("IDb"), scale=c)
+    act(QN, Q0, scale=-16384.0, bias=16384.0)
+    act(Q2, QC, scale=2.0)
+    act(R("TT0"), R("NM0", 0, 512), scale=Q0, bias=QN)
+    select(R("TMS"), R("BOS"), ALU.is_gt, 0.0)
+    select(R("TMS"), R("TMS"), ALU.not_equal, -float(1 << 21))
+    iota(R("NM1"), [[0, 2], [2, 512]], r * V + 2, 0)
+    iota(R("DN8"), [[1, 2], [32, 32]], 0, 0)
+    iota(R("slot"), [[16, 112]], 0, 0)
+    iota(R("TP"), [[256, W]], 0, 0)
+    dma("G", R("TP", 0, V), T.toll[:, 0:V], add=True)
+    dma("G", R("TP", V, W), T.toll[:, V:W], add=True)
+
+    def shuffle(out, pi, e, first):
+        for hh in range(2):
+            k = 2 * pi + hh
+            mm(out, R("SHF", 128 * k, 128 * k + 128), R("nbf", 2 * e + hh, 512, 4), first and hh == 0, hh == 1)
+
+    def lists(pi):
+        for e in range(2):
+            shuffle(R("ps%d" % (4 + 3 * pi), 128 * e, 128 * e + 128), pi, e, True)
+
+    def lists_out(pi, name):
+        for e in range(2):
+            o, src = R(name, 256 * pi + e, 256 * pi + 256, 2), R("ps%d" % (4 + 3 * pi), 128 * e, 128 * e + 128)
+            if name == "L0":
+                ts(o, src, float(V), ALU.min)
+            else:
+                copy(o, src)
+
+    lists(0)
+    lists(1)
+    copy(R("B0", 0, 512), R("pathi", 0, 512))
+    lists_out(0, "L0")
+    copy(R("B0", 512, V), R("pathi", 512, V))
+
+    def link_prep():
+        for e in range(2):
+            copy(R("Xb", 256 * e, 256 * e + 256), R4("X", e))
+        act(R("DNb"), R("Xb"), scale=1.0 / 16, bias=192.0 - 15.0 / 32)
+        for e in range(2):
+            copy(R("Ob", 256 * e, 256 * e + 256, p1=16), R4("O", e, 16))
+        ts(R("R16", p1=16), R("RQ", p1=16), R("col", 1, 2, p1=16), ALU.is_equal, -256.0, ALU.mult)
+
+    def link_tables(pi):
+        for e in range(2):
+            o = R("ps5", 128 * e, 128 * e + 128)
+            ob = R("Ob", 256 * e + pi, 256 * e + 256, 2, p1=16)
+            mm(o, R("Xb", 256 * e + pi, 256 * e + 256, 2), R("IDb"), True, False)
+            mm(o, ob, R("R16", p1=16), False, True)
+            mm(R("ps5", 256 + 16 * e, 272 + 16 * e), ob, R("IDb", 0, 16, p1=16), True, True)
+        for e in range(2):
+            o = R("ps6", 128 * e, 128 * e + 128)
+            mm(o, R("Xb", 256 * e + pi, 256 * e + 256, 2), R("I20"), True, False)
+            mm(o, R("DNb", 256 * e + pi, 256 * e + 256, 2), R("NEG"), False, False)
+            mm(o, R("ONE"), R("I192"), False, False)
+            mm(o, R("ONE"), R("DK"), False, False)
+            shuffle(o, pi, e, False)
+
+    def link_tables_out(pi):
+        for e in range(2):
+            act(R("LK", 256 * pi + e, 256 * pi + 256, 2), R("ps5", 128 * e, 128 * e + 128))
+        for e in range(2):
+            act(R("CST", 256 * pi + e, 256 * pi + 256, 2), R("ps6", 128 * e, 128 * e + 128))
+        for e in range(2):
+            src = R("ps5", 256 + 16 * e, 272 + 16 * e)
+            if pi == 0:
+                act(R("DP0", e, 32, 2), src, bias=float(V))
+            act(R("DP", 64 * pi + e, 64 * pi + 32, 2), src, bias=float(W))
+
+    def down(t, pi):
+        ts(R("DT%d" % t, 256 * pi, 256 * pi + 256), R("LK", 256 * pi, 256 * pi + 256), 16.0 * (t + 1), ALU.is_lt, 1.0, ALU.add)
+
+    def path_constants():
+        ts(C2, Q0, R("ZT", 1, 2), ALU.add, 16384.0, ALU.mult)
+        ts(R("SHT"), R("DD"), -1.0, ALU.is_equal)
+        lists_out(1, "L0")
+        ts(R("SHT", 0, 128, 16), R("RG", 0, 128, 16), GC, ALU.is_equal, C2, ALU.mult)
+        lists_out(1, "L")
+
+    def crossing_constants():
+        copy(R("shu"), R("shi"))
+        memset(R("RST"), 1.0)
+        memset(R("C191"), 191.0 / 16)
+        memset(R("B1", 0, 8), 0.0)
+        memset(R("RST", 0, 112, 16), 0.0)
+        ts(R("SA0"), R("shi"), 8.0, ALU.add)
+
+    def more_constants():
+        for pi in range(2):
+            ts(R("DN", 64 * pi, 64 * pi + 32), R("DN8", 32 * pi, 32 * pi + 32), Q2, ALU.add)
+        ts(R("DN8"), R("DN8"), Q2, ALU.add, 8192.0, ALU.add)
+        act(R("SA1"), R("SA0"), bias=float(GH - 8))
+        act(R("slot"), R("slot"), bias=QC)
+        for t in (1, 2, 3):
+            act(R("B%d" % t, PRE[t] + W, PRE[t] + W + 8), R("ZT"))
+        copy(R("atu"), R("ati"))
+        ts(R("MPK", 15, 143, 16), R("RG", 0, 128, 16), GC, ALU.is_equal, Q0, ALU.mult)
+
+    def window(t):
+        return R("B%d" % t, PRE[t], PRE[t] + (V if t == 0 else W) + 8)
+
+    def offsets(t, pi, c, lo=0, hi=64):
+        return R("L0" if t == 0 else "L", 256 * pi + 64 * c + lo, 256 * pi + 64 * c + hi)
+
+    def loops(t, pi, c, lo=0, hi=64):
+        tt(R("EQ", V * c + 16 * lo, V * c + 16 * hi), IND(window(t), offsets(t, pi, c, lo, hi)), R("NM%d" % pi, 16 * lo, 16 * hi), ALU.is_equal)
+
+    def filled(t, pi, c):
+        act(R("SG", V * c, V * c + V), IND(window(t), offsets(t, pi, c)), ACT.Sign)
+
+    def scores(t, pi, c, part="all", bank=0):
+        o = R("ps%d" % (bank + c), 0, 64)
+        lo = 256 * pi + 64 * c
+        if part != "close":
+            for q in range(16):
+                mm(o, R("MSG", 15 - q, 143 - q), R("SG", V * c + q, V * c + V, 16), q == 0, False)
+        if part == "all":
+            mm(o, R("NEG"), R("DT%d" % t, lo, lo + 64), False, False)
+        if part != "close":
+            for q in range(16):
+                mm(o, R("MEQ", 15 - q, 143 - q), R("EQ", V * c + q, V * c + V, 16), False, False)
+        if part == "close":
+            mm(o, R("NEG"), R("DT%d" % t, lo, lo + 64), False, False)
+        if part != "open":
+            mm(o, R("IDf"), R("CST", lo, lo + 64), False, True)
+
+    def running(t, pi, c, crit, bank=0):
+        base = 0 if crit else 256
+        if c == 0:
+            prev = R(("DP0" if t == 0 else "DP") if crit else "DN", 64 * pi, 64 * pi + 64)
+        else:
+            prev = R("RUN", base + 64 * c - 64, base + 64 * c)
+        tt(R("RUN", base + 64 * c, base + 64 * c + 64), R("ps%d" % (bank + c), 0, 64), prev, ALU.max)
+
+    def nh_list(t, pi):
+        return R("NH", 64 * t + 32 * pi, 64 * t + 32 * pi + 32)
+
+    def winners(t, pi, crit, bank=0):
+        running(t, pi, 3, crit, bank)
+        base = 192 if crit else 448
+        k = 0 if crit else 32
+        tt(R("RI", k, k + 32), R("RUN", base, base + 32), R("RUN", base + 32, base + 64), ALU.max)
+        ts(R("RA", k, k + 32), R("RI", k, k + 32), 4095, ALU.bitwise_and)
+        copy(R("PL", 32 * t, 32 * t + 32) if crit else nh_list(t, pi), R("RA", k, k + 32))
+
+    def choice(t, pi, crit, early=0, done=0, fill=None):
+        for c in range(4):
+            if c >= done:
+                loops(t, pi, c)
+            if c >= early:
+                filled(t, pi, c)
+            if ("a", c) in fill:
+                fill[("a", c)]()
+            scores(t, pi, c)
+            if c == 3:
+                for k in range(3):
+                    running(t, pi, k, crit)
+            if c in fill:
+                fill[c]()
+        winners(t, pi, crit)
+
+    def first_choice():
+        loops(0, 0, 0)
+        filled(0, 0, 0)
+        link_prep()
+        scores(0, 0, 0, "open")
+        link_tables(0)
+        loops(0, 0, 1)
+        filled(0, 0, 1)
+        link_tables_out(0)
+        scores(0, 0, 1, "open")
+        loops(0, 0, 2)
+        filled(0, 0, 2)
+        down(0, 0)
+        scores(0, 0, 0, "close")
+        scores(0, 0, 1, "close")
+        scores(0, 0, 2)
+        loops(0, 0, 3)
+        filled(0, 0, 3)
+        scores(0, 0, 3)
+        carry(0, 1)
+        act(R("TT1"), R("NM1", 0, 512), scale=Q0, bias=QN)
+        path_constants()
+        for c in range(3):
+            running(0, 0, c, True)
+        winners(0, 0, True)
+        dma("Y", R("tg"), T.toll[:, V:W])
+        dma("Y", R("H", V, W), R("TP", V, W))
+
+    def crit_nh(t):
+        pi = t & 1
+        tt(R("NI"), R("RI", 0, 32), R("DN8", 32 * pi, 32 * pi + 32), ALU.max)
+        ts(R("NA"), R("NI"), 4095, ALU.bitwise_and)
+        copy(nh_list(t, pi), R("NA"))
+
+    def path_gather(t, hf, on_v, bank=2):
+        out = R("PG", 256 * hf, 256 * hf + 256)
+        move(out, IND(window(t), R("PL", 32 * t + 16 * hf, 32 * t + 16 * hf + 16)), on_v)
+        mm(R("ps%d" % (bank + hf), 0, 256), R("SHT"), out, True, True)
+
+    def path_store(t, hf, bank=2):
+        pi = t & 1
+        lo = PRE[t + 1] + 512 * hf
+        tt(R("B%d" % (t + 1), lo + pi, lo + 512, 2), R("ps%d" % (bank + hf), 0, 256), R("TT%d" % pi, 256 * hf, 256 * hf + 256), ALU.min)
+
+    def carry(t, pi):
+        act(R("B%d" % (t + 1), PRE[t + 1] + pi, PRE[t + 1] + V, 2), R("B%d" % t, PRE[t] + pi, PRE[t] + V, 2))
+
+    def masks(ch):
+        out, k = {}, 0
+        for d in ch:
+            if d in near:
+                es = [e for e in topo.engines(core, dest[d]) if e not in far_engines][:share]
+            else:
+                es = far_engines[k * share:(k + 1) * share]
+                k += 1
+            out[d] = sum(1 << e for e in es)
+        return out
+
+    def last_buf(t):
+        return "SND" if t == 2 else "B%d" % (t + 2)
+
+    def span(j):
+        return 16 * order.index(chunks[j][0]), 16 * order.index(chunks[j][-1]) + 16
+
+    def differ(t, j, on_v=True):
+        m0, m1 = span(j)
+        b = "B%d" % (t + 1)
+        src = IND(R(b, PRE[t + 1], PRE[t + 1] + V), R("shu", m0, m1))
+        out = R("NE", 16 * m0, 16 * m1)
+        if t > 0:
+            tt(out, src, R(b, 16 * m0, 16 * m1), ALU.not_equal)
+        elif on_v:
+            ts(out, src, 0.0, ALU.not_equal)
+        else:
+            act(out, src, ACT.Sign)
+        for q in range(16):
+            mm(R("ps%d" % (6 + (j & 1)), 0, m1 - m0), R("MEQ", 15 - q, 143 - q), R("NE", 16 * m0 + q, 16 * m1, 16), q == 0, q == 15)
+
+    def count(t, j):
+        m0, m1 = span(j)
+        o, a, b = R("SC", m0, m1), R("RST", m0, m1), R("CH", m0, m1)
+        ts(b, R("ps%d" % (6 + (j & 1)), 0, m1 - m0), 0.0, ALU.is_lt, -1.0, ALU.mult)
+        add_op(pl, "V", lambda h: h.tensor_tensor_scan(o[0], a[0], b[0], 0.0, ALU.mult, ALU.subtract), [a, b], [o])
+        ps = R("ps%d" % (j & 1), 0, m1 - m0)
+        mm(ps, R("BOS"), R("C191", m0, m1), True, False)
+        mm(ps, R("TMS"), b, False, False)
+        mm(ps, R("BOS"), o, False, True)
+
+    def pick(t, j, split):
+        m0, m1 = span(j)
+        tt(R("M1", m0, m1), R("ps%d" % (j & 1), 0, m1 - m0), R("SA0" if t == 0 else "SA1", m0, m1), ALU.min)
+        if t == 0:
+            copy(R("XI", m0, m1), R("M1", m0, m1))
+        else:
+            tt(R("M2", m0, m1), R("M1", m0, m1), R("slot", m0, m1), ALU.max)
+            copy(R("XI", m0, m1), R("M2", m0, m1))
+        win = R("B%d" % (t + 1), 0, PRE[t + 1] + V)
+        mid = (m0 + m1) // 2 if split else m1
+        act(R(last_buf(t), 16 * m0, 16 * mid), IND(win, R("XI", m0, mid)))
+        if split:
+            copy(R(last_buf(t), 16 * mid, 16 * m1), IND(win, R("XI", mid, m1)))
+        mk = masks(chunks[j])
+        trs = []
+        for d in chunks[j]:
+            rid, pid, se = topo.addr(dest[d])
+            lo, at = PRE[t + 1] + V + G * (d - 1), G * order.index(d)
+            trs.append(RemoteDMATransfer(dst_ids=[DstId(rid=rid, pnc=pid)], dma_engine_mask=mk[d], remote_sem=T.sem["arr%d" % t],
+                                         src=T[last_buf(t)][:, at:at + G], dst=T["B%d" % (t + 1)][:, lo:lo + G]))
+        add_op(pl, "G", lambda h: h.remote_dma_fused(trs, local_sem=T.sem.sent), [R(last_buf(t), 16 * m0, 16 * m1)], [],
+               sem="sent", inc=share * len(trs))
+
+    def crossing(t):
+        differ(t, 0)
+        differ(t, 1, on_v=t > 0)
+        if t == 0:
+            filled(0, 1, 0)
+        count(t, 0)
+        if t == 0:
+            differ(t, 2)
+        pick(t, 0, False)
+        if t > 0:
+            differ(t, 2)
+        count(t, 1)
+        pick(t, 1, False)
+        count(t, 2)
+        pick(t, 2, True)
+        add_op(pl, "X", None, [], [R("B%d" % (t + 1), PRE[t + 1] + V, PRE[t + 1] + W)], sem="arr%d" % t, inc=share * (N - 1))
+
+    def hop_table(t, pi, lo=0, hi=32, on_v=False):
+        k = 64 * t + 32 * pi
+        move(R("A" if t == 0 else "H", 32 * lo + pi, 32 * hi, 2), IND(R("TP"), R("NH", k + lo, k + hi)), on_v)
+
+    def follow(t):
+        for k in range(2):
+            if t == 1:
+                act(R("X1", k, V, 2), IND(R("H"), nh_list(0, k)))
+            else:
+                move(R("X2", 512 * k, 512 * k + 512), IND(R("H"), R("Q1", 32 * k, 32 * k + 32)), k == 0)
+
+    def follow_turn(t):
+        x = "X%d" % t
+        for q in range(16):
+            mm(R("ps5", 0, 64), R("MPK", 15 - q, 143 - q), R(x, q, V, 16), q == 0, q == 15)
+        dma("G", R("A"), R(x), add=True)
+
+    def follow_list(t):
+        copy(R("QI"), R("ps5", 0, 64))
+        ts(R("QA"), R("QI"), 8, ALU.arith_shift_right)
+        copy(R("Q%d" % t), R("QA"))
+
+    def ghost_floor():
+        act(R("FL"), R("tg"), scale=1.0 / 64, bias=192.0 - 63.0 / 128)
+
+    def ghost_sums():
+        for k in range(4):
+            lo = 448 * k
+            mm(R("ps%d" % (4 + k), 0, 448), R("I4"), R("tg", lo, lo + 448), True, False)
+            mm(R("ps%d" % (4 + k), 0, 448), R("I256"), R("FL", lo, lo + 448), False, True)
+
+    def ghost_sums_out():
+        for k in range(4):
+            act(R("FW", V + 448 * k, V + 448 * k + 448), R("ps%d" % (4 + k), 0, 448), bias=49152.0)
+
+    for t in range(RO - 1):
+        pi = t & 1
+        if t == 0:
+            first_choice()
+        else:
+            choice(t, pi, True, fill={3: lambda: loops(t, 1 - pi, 0, 0, 32)})
+        path_gather(t, 0, False)
+        path_gather(t, 1, True)
+        if t == 0:
+            crossing_constants()
+        else:
+            loops(t, 1 - pi, 0, 32, 64)
+        path_store(t, 0)
+        path_store(t, 1)
+        if t > 0:
+            filled(t, 1 - pi, 0)
+            filled(t, 1 - pi, 1)
+        crossing(t)
+        if t == 0:
+            link_tables(1)
+            link_tables_out(1)
+            more_constants()
+            lists_out(0, "L")
+            down(0, 1)
+        crit_nh(t)
+        down(t + 1, 1 - pi)
+        down(t + 1, pi)
+
+        def packets():
+            carry(t + 1, pi)
+            if t == 2:
+                hop_table(1, 0)
+                follow(1)
+            hop_table(t, pi)
+            if t == 0:
+                ghost_floor()
+            if t == 1:
+                ghost_sums_out()
+
+        fill = {("a", 3): packets}
+        if t == 1:
+            fill[0] = ghost_sums
+        if t == 2:
+            fill[3] = lambda: follow_turn(1)
+        choice(t, 1 - pi, False, 1 if t == 0 else 2, 0 if t == 0 else 1, fill)
+        if t != 1:
+            hop_table(t, 1 - pi, on_v=True)
+    follow_list(1)
+    follow(2)
+    follow_turn(2)
+
+    for pi in (1, 0):
+        for c in range(4):
+            loops(3, pi, c)
+            filled(3, pi, c)
+            scores(3, pi, c, "all", 0 if pi else 4)
+            if pi == 1 and c == 3:
+                follow_list(2)
+            if pi == 0 and c == 1:
+                for k in range(3):
+                    running(3, 1, k, True)
+                winners(3, 1, True)
+                crit_nh(3)
+    path_gather(3, 0, False, 0)
+    path_gather(3, 1, False, 0)
+    hop_table(3, 1, on_v=True)
+    for k in range(3):
+        running(3, 0, k, False, 4)
+    winners(3, 0, False, 4)
+    hop_table(3, 0, 0, 16)
+    hop_table(3, 0, 16, 32, on_v=True)
+    tt(R("ZI"), IND(R("H"), R("Q2")), R("A"), ALU.add)
+    for hf in range(2):
+        path_store(3, hf, 0)
+        dma("Y", T.ypath[:, 512 * hf:512 * hf + 512], R("B4", 512 * hf, 512 * hf + 512))
+    ts(R("ZA"), R("ZI"), 255, ALU.bitwise_and)
+    copy(R("FW", 0, V), R("ZA"))
+    for k in range(4):
+        lo = 512 * k
+        move(R("YS", lo, lo + 512), IND(R("FW"), R("atu", 32 * k, 32 * k + 32)), k & 1 == 0)
+        dma("Y", T.ysum[:, lo:lo + 512], R("YS", lo, lo + 512))
+    emit(pl, g, T)

@@ -1,11 +1,15 @@
+import math
 from concourse.bass import DstId, RemoteDMATransfer
 from concourse.mybir import AluOpType as ALU, ActivationFunctionType as ACT
 
 N, V, G, W, P, RO = 8, 1024, 256, 2816, 2048, 4
 GH = W - V
 BIG = float(1 << 24)
-PRE = (0, 8, GH, GH, 0)
+PRE = (0, 16, GH, GH)
 F32, BF, I32, U16 = "float32", "bfloat16", "int32", "uint16"
+STEP, BASE, MID = 0.00885, math.log(255.0), 3283
+RND = 12582912.0
+CFG = {"g": 1.3, "hop": 0.13, "fly": 4.0, "dma": 2.2, "pe": 0.00045, "crit_v": (0,), "non_v": (), "direct": ()}
 
 
 def _sb(n, dt):
@@ -13,91 +17,119 @@ def _sb(n, dt):
 
 
 SCRATCH = {
-    "B0": _sb(V + 8, F32), "B1": _sb(8 + W + 8, F32), "B2": _sb(GH + W + 8, F32), "B3": _sb(GH + W + 8, F32),
-    "B4": _sb(V, F32), "SND": _sb(GH, F32),
-    "pathi": _sb(V, I32), "nbi": _sb(512, I32), "nbf": _sb(512, F32),
+    "B0": _sb(V + 16, BF), "B1": _sb(16 + W + 16, BF), "B2": _sb(GH + W + 16, BF), "B3": _sb(GH + W + 16, BF),
+    "SND": _sb(GH, BF), "YP": _sb(V, F32), "YE": _sb(512, BF), "YL": _sb(512, F32), "YR": _sb(512, F32),
+    "pathi": _sb(V, I32), "PF": _sb(V, F32), "FLG": _sb(V, BF), "EN": _sb(V, BF), "nbi": _sb(512, I32), "nbf": _sb(512, F32),
     "X": ("sbuf", [128, 8, 2, 32], I32), "O": ("sbuf", [128, 8, 2, 32], I32),
     "Xb": _sb(512, BF), "DNb": _sb(512, BF), "Ob": _sb(512, BF),
     "shi": _sb(112, I32), "shu": _sb(112, U16), "SA0": _sb(112, F32), "SA1": _sb(112, F32), "slot": _sb(112, F32),
     "ati": _sb(128, I32), "atu": _sb(128, U16),
-    "kci": _sb(4, I32), "gqi": _sb(4, I32), "col": _sb(16, F32),
+    "kci": _sb(4, I32), "gqi": _sb(4, I32), "col": _sb(32, F32),
     "SV": _sb(128, F32), "RG": _sb(128, F32), "DD": _sb(128, F32), "RQ": _sb(128, F32),
-    "SHF": _sb(512, F32), "IDb": _sb(128, BF), "IDf": _sb(128, F32), "NEG": _sb(128, BF), "I20": _sb(128, BF),
-    "DK": _sb(128, BF), "ONE": _sb(128, BF), "R16": _sb(128, BF), "I192": _sb(128, BF),
-    "MEQ": _sb(144, BF), "MSG": _sb(144, BF), "MPK": _sb(144, F32), "SHT": _sb(128, F32),
+    "SHF": _sb(512, F32), "IDb": _sb(128, BF), "IDf": _sb(128, F32), "NEG": _sb(128, BF), "I19": _sb(128, BF), "N23": _sb(128, BF),
+    "DK": _sb(128, BF), "ONE": _sb(256, BF), "R16": _sb(128, BF), "I192": _sb(128, BF), "D1": _sb(128, BF), "D2": _sb(128, BF), "D15": _sb(128, BF),
+    "MEQ": _sb(144, BF), "MM": _sb(144, BF), "MNE": _sb(144, BF), "MPK": _sb(144, F32), "SHT": _sb(128, BF), "SHU": _sb(128, BF),
     "BOS": _sb(128, BF), "TMS": _sb(128, BF), "C191": _sb(112, BF), "RST": _sb(112, BF),
-    "NM0": _sb(V, F32), "NM1": _sb(V, F32), "TT0": _sb(512, F32), "TT1": _sb(512, F32), "ZT": _sb(8, F32),
+    "NF0": _sb(512, F32), "NF1": _sb(512, F32), "NM0": _sb(512, BF), "NM1": _sb(512, BF), "TT0": _sb(512, BF), "TT1": _sb(512, BF), "ZT": _sb(16, BF),
     "L0": _sb(512, U16), "L": _sb(512, U16), "CST": _sb(512, F32), "LK": _sb(512, BF),
     "DT0": _sb(512, BF), "DT1": _sb(512, BF), "DT2": _sb(512, BF), "DT3": _sb(512, BF),
-    "DP0": _sb(64, F32), "DP": _sb(128, F32), "DN": _sb(128, F32), "DN8": _sb(64, F32),
-    "EQ": _sb(4096, BF), "SG": _sb(4096, BF), "RUN": _sb(512, F32),
+    "DP0": _sb(64, F32), "DP": _sb(128, F32), "DN": _sb(256, F32), "DN8": _sb(64, F32),
+    "EQ0": _sb(4096, BF), "GA0": _sb(4096, BF), "EQ1": _sb(4096, BF), "GA1": _sb(4096, BF), "EQ2": _sb(4096, BF), "GA2": _sb(4096, BF),
+    "RUN": _sb(256, F32), "RUN2": _sb(384, F32),
     "RI": _sb(64, I32), "RA": _sb(64, I32), "NI": _sb(32, I32), "NA": _sb(32, I32), "PL": _sb(128, U16), "NH": _sb(256, U16),
-    "PG": _sb(512, F32),
+    "PG": _sb(512, BF),
     "NE": _sb(GH, BF), "CH": _sb(112, BF), "SC": _sb(112, BF), "M1": _sb(112, F32), "M2": _sb(112, F32), "XI": _sb(112, U16),
-    "TP": _sb(W, F32), "H": _sb(W, F32), "A": _sb(V, F32), "X1": _sb(V, F32), "X2": _sb(V, F32),
-    "QI": _sb(64, I32), "QA": _sb(64, I32), "Q1": _sb(64, U16), "Q2": _sb(64, U16),
-    "tg": _sb(GH, BF), "FL": _sb(GH, BF), "I4": _sb(128, BF), "I256": _sb(128, BF), "FW": _sb(W, BF),
+    "TL": _sb(W, BF), "TP": _sb(W, F32), "U2": _sb(W, F32), "U1": _sb(V, F32), "T0": _sb(V, F32), "H": _sb(W, BF),
+    "QI": _sb(64, I32), "QA": _sb(64, I32), "Q": _sb(64, U16),
+    "FL": _sb(GH, BF), "I4": _sb(128, BF), "I256": _sb(128, BF), "FW": _sb(W, BF),
     "ZI": _sb(V, I32), "ZA": _sb(V, I32), "YS": _sb(P, BF),
 }
 for _b in range(8):
     SCRATCH["ps%d" % _b] = ("psum", [128, 512], F32)
 
-SEMAPHORES = ["qV", "qS", "qP", "qG", "sent", "arr0", "arr1", "arr2"] + ["d%d" % _b for _b in range(32)]
-
-
-def add_op(pl, q, fn, reads, writes, sem=None, inc=16):
-    pl["ops"].append({"q": q, "fn": fn, "r": reads, "w": writes, "sem": sem, "inc": inc})
+SEMAPHORES = ["qV", "qS", "qP", "qG", "sent", "arr0", "arr1", "arr2"] + ["d%d" % _b for _b in range(60)]
 
 
 def overlap(a, b):
     return a[1].startswith("ps") or (a[2] < b[3] and b[2] < a[3])
 
 
-def emit(pl, g, T):
-    ops = pl["ops"]
-    queues = {"V": g.vector, "S": g.scalar, "P": g.tensor, "G": g, "Y": g.sync}
-    total = {}
-    for o in ops:
-        if o["sem"] is not None:
-            total[o["sem"]] = total.get(o["sem"], 0) + o["inc"]
-    known = {q: {} for q in queues}
+def depend(ops):
     touch = {}
     for n, o in enumerate(ops):
-        q = o["q"]
-        o["key"] = o["sem"] if o["sem"] is not None else "q" + q
         accs = [(a, False) for a in o["r"]] + [(a, True) for a in o["w"]]
-        deps = set()
+        deps = set(o["after"])
         for acc, wr in accs:
             for (m, b, bw) in touch.get(acc[1], []):
-                e = ops[m]
-                if overlap(acc, b) and not (q == "P" and e["q"] == "P") and (wr or bw or (acc[1].startswith("ps") and e["q"] != q)):
+                if overlap(acc, b) and (wr or bw or (acc[1].startswith("ps") and ops[m]["q"] != o["q"])):
                     deps.add(m)
         for acc, wr in accs:
             touch.setdefault(acc[1], []).append((n, acc, wr))
-        o["waits"] = []
-        if q == "X":
-            o["vc"] = {o["key"]: len(ops)}
-            continue
-        kn = known[q]
-        for m in sorted(deps, reverse=True):
+        o["deps"] = deps
+
+
+def arrange(ops):
+    rank = [0.0] * len(ops)
+    for n in range(len(ops) - 1, -1, -1):
+        rank[n] += ops[n]["cost"] + ops[n]["late"] + CFG["hop"]
+        for m in ops[n]["deps"]:
+            rank[m] = max(rank[m], rank[n])
+    taken = {}
+    for n in sorted(range(len(ops)), key=lambda k: (-1e9 if ops[k]["sem"] and not ops[k]["deps"] else -rank[k], k)):
+        o = ops[n]
+        t = 0.0
+        for m in o["deps"]:
             e = ops[m]
-            if (e["sem"] is not None and e["sem"] == o["sem"]) or kn.get(e["key"], -1) >= m:
+            t = max(t, e["end"] + (0.0 if e["q"] == "P" and o["q"] == "P" else CFG["hop"]))
+        spans = taken.setdefault(o["q"], [])
+        k = 0
+        while k < len(spans) and (spans[k][1] <= t or spans[k][0] < t + o["cost"]):
+            t = max(t, spans[k][1])
+            k += 1
+        spans.insert(k, (t, t + o["cost"]))
+        o["start"], o["end"] = t, t + o["cost"] + o["late"]
+    return sorted(range(len(ops)), key=lambda k: (ops[k]["start"], k))
+
+
+def emit(ops, g, T):
+    depend(ops)
+    order = arrange(ops)
+    queues = {"V": g.vector, "S": g.scalar, "P": g.tensor, "G": g, "Y": g.sync}
+    total = {}
+    for k, n in enumerate(order):
+        o = ops[n]
+        o["at"] = k
+        o["key"] = o["sem"] if o["sem"] is not None else "q" + o["q"]
+        if o["sem"] is not None:
+            total[o["sem"]] = total.get(o["sem"], 0) + o["inc"]
+    known = {q: {} for q in queues}
+    for n in order:
+        o = ops[n]
+        o["waits"] = []
+        if o["q"] == "X":
+            o["vc"] = {o["key"]: o["at"]}
+            continue
+        kn = known[o["q"]]
+        for m in sorted(o["deps"], key=lambda k: -ops[k]["at"]):
+            e = ops[m]
+            if (e["q"] == "P" and o["q"] == "P") or kn.get(e["key"], -1) >= e["at"]:
                 continue
             o["waits"].append(m)
             e["need"] = True
-            for x in ([e] if e["sem"] is None else [x for x in ops[:n] if x["sem"] == e["sem"]]):
-                for k, val in x["vc"].items():
-                    if kn.get(k, -1) < val:
-                        kn[k] = val
+            for k, val in e["vc"].items():
+                if kn.get(k, -1) < val:
+                    kn[k] = val
         o["vc"] = dict(kn)
-        o["vc"][o["key"]] = len(ops) if o["sem"] is not None else n
+        o["vc"][o["key"]] = o["at"]
     count = {}
-    for o in ops:
+    for n in order:
+        o = ops[n]
         if o["sem"] is None and o.get("need"):
             count[o["key"]] = count.get(o["key"], 0) + 1
             o["val"] = count[o["key"]]
     waited = set()
-    for o in ops:
+    for n in order:
+        o = ops[n]
         if o["q"] == "X":
             continue
         h = queues[o["q"]]
@@ -123,54 +155,67 @@ def rank_program(g, core, T, topo):
     r = T.rank_of(core)
     if r is None:
         return
-    pl = {"ops": [], "dma": {}, "ndma": [0]}
+    ops = []
+    ndma = [0]
+
+    def add(q, fn, reads, writes, cost, late=0.0, sem=None, inc=16, after=()):
+        ops.append({"q": q, "fn": fn, "r": reads, "w": writes, "cost": cost, "late": late, "sem": sem, "inc": inc, "after": after})
+        return len(ops) - 1
 
     def R(name, lo=0, hi=None, step=1, p1=128):
         t = T[name]
         if hi is None:
             hi = t.shape[1]
-        return (t[0:p1, lo:hi] if step == 1 else t[0:p1, lo:hi:step], name, lo, hi)
+        return (t[0:p1, lo:hi] if step == 1 else t[0:p1, lo:hi:step], name, lo, hi, (hi - lo + step - 1) // step)
 
     def R4(name, e, rows=128):
-        return (T[name][0:rows, :, e, :], name, 0, 512)
+        return (T[name][0:rows, :, e, :], name, 0, 512, 256)
 
     def IND(win, off):
-        return (win[0].indirect(off[0]), win[1], win[2], win[3], off)
+        return (win[0].indirect(off[0]), win[1], win[2], win[3], 16 * off[4], off)
 
     def rd(*aps):
         out = []
         for a in aps:
             if isinstance(a, tuple):
                 out.append(a)
-                if len(a) == 5:
-                    out.append(a[4])
+                if len(a) == 6:
+                    out.append(a[5])
         return out
 
     def val(a):
         return a[0] if isinstance(a, tuple) else a
 
+    def price(out, a, rate=1.0, fast=True):
+        if len(a) == 6:
+            return 0.08 + a[4] * CFG["g"] * 0.00083
+        if fast and SCRATCH[out[1]][2] in (BF, U16) and SCRATCH[a[1]][2] in (BF, U16):
+            rate = 0.5
+        return 0.03 + max(64, a[4] * rate) * 0.00083
+
     def copy(out, in_):
-        add_op(pl, "V", lambda h: h.tensor_copy(out[0], in_[0]), rd(in_), [out])
+        add("V", lambda h: h.tensor_copy(out[0], in_[0]), rd(in_), [out], price(out, in_))
 
     def tt(out, a, b, op):
-        add_op(pl, "V", lambda h: h.tensor_tensor(out[0], a[0], b[0], op), rd(a, b), [out])
+        one = a[1].startswith("ps") or b[1].startswith("ps")
+        add("V", lambda h: h.tensor_tensor(out[0], a[0], b[0], op), rd(a, b), [out], price(out, a, 1.0 if one else 2.0, False))
 
     def ts(out, a, s1, op0, s2=None, op1=None):
         if op1 is None:
-            add_op(pl, "V", lambda h: h.tensor_scalar(out[0], a[0], val(s1), None, op0), rd(a, s1), [out])
+            add("V", lambda h: h.tensor_scalar(out[0], a[0], val(s1), None, op0), rd(a, s1), [out], price(out, a))
         else:
-            add_op(pl, "V", lambda h: h.tensor_scalar(out[0], a[0], val(s1), val(s2), op0, op1), rd(a, s1, s2), [out])
+            add("V", lambda h: h.tensor_scalar(out[0], a[0], val(s1), val(s2), op0, op1), rd(a, s1, s2), [out], price(out, a))
 
     def memset(out, c):
-        add_op(pl, "V", lambda h: h.memset(out[0], c), [], [out])
+        add("V", lambda h: h.memset(out[0], c), [], [out], price(out, out))
 
-    def act(out, a, func=ACT.Identity, scale=None, bias=None):
+    def act(out, a, func=ACT.Identity, scale=None, bias=None, more=0.0):
         kw = {}
         if scale is not None:
             kw["scale"] = val(scale)
         if bias is not None:
             kw["bias"] = val(bias)
-        add_op(pl, "S", lambda h: h.activation(out[0], a[0], func, **kw), rd(a, scale, bias), [out])
+        add("S", lambda h: h.activation(out[0], a[0], func, **kw), rd(a, scale, bias), [out], price(out, a, 1.0, False) + more)
 
     def move(out, in_, on_v):
         if on_v:
@@ -178,30 +223,34 @@ def rank_program(g, core, T, topo):
         else:
             act(out, in_)
 
-    def mm(out, lhsT, rhs, start, stop):
-        add_op(pl, "P", lambda h: h.matmul(out[0], lhsT[0], rhs[0], start, stop), [lhsT, rhs], [out])
+    def mms(calls):
+        def fn(h):
+            for o, l, x, a, b in calls:
+                ins = h.matmul(o[0], l[0], x[0], a, b)
+            return ins
+        cost = sum(max(64, x[4]) * (4 if SCRATCH[x[1]][2] == F32 else 1) for o, l, x, a, b in calls) * CFG["pe"]
+        add("P", fn, [c[1] for c in calls] + [c[2] for c in calls], [c[0] for c in calls], cost)
+
+    def turn(out, sel, buf, lo, hi, start, stop):
+        mms([(out, R(sel, 15 - q, 143 - q), R(buf, lo + q, hi, 16), start and q == 0, stop and q == 15) for q in range(16)])
 
     def iota(out, pattern, base, cm, flt=True):
+        cost = 0.15 + out[4] * 0.00166
         if flt:
-            add_op(pl, "G", lambda h: h.iota(out[0], pattern, base, cm, allow_small_or_imprecise_dtypes=True), [], [out])
+            add("G", lambda h: h.iota(out[0], pattern, base, cm, allow_small_or_imprecise_dtypes=True), [], [out], cost)
         else:
-            add_op(pl, "G", lambda h: h.iota(out[0], pattern, base, cm), [], [out])
+            add("G", lambda h: h.iota(out[0], pattern, base, cm), [], [out], cost)
 
     def select(out, in_, op, fill):
-        add_op(pl, "G", lambda h: h.affine_select(out[0], in_[0], [[-1, 128]], op, fill, 0, 1), [in_], [out])
+        add("G", lambda h: h.affine_select(out[0], in_[0], [[-1, 128]], op, fill, 0, 1), [in_], [out], 0.4)
 
-    def dma(q, out, in_, grp=None, add=False):
-        if grp not in pl["dma"]:
-            s = "d%d" % pl["ndma"][0]
-            pl["ndma"][0] += 1
-            if grp is not None:
-                pl["dma"][grp] = s
-        else:
-            s = pl["dma"][grp]
-        if add:
-            add_op(pl, q, lambda h: h.dma_start(val(out), val(in_), accum_op=ALU.add), rd(in_, out), rd(out), sem=s)
-        else:
-            add_op(pl, q, lambda h: h.dma_start(val(out), val(in_)), rd(in_), rd(out), sem=s)
+    def dma(q, out, in_, adding=False, late=None, after=()):
+        s = "d%d" % ndma[0]
+        ndma[0] += 1
+        late = CFG["dma"] if late is None else late
+        if adding:
+            return add(q, lambda h: h.dma_start(val(out), val(in_), accum_op=ALU.add), rd(in_, out), rd(out), 1.0, late + 1.0, s, after=after)
+        return add(q, lambda h: h.dma_start(val(out), val(in_)), rd(in_), rd(out), 0.06, late, s, after=after)
 
     here = topo.chip(core)
     dest = {d: T.cores[(r + d) % N] for d in range(1, N)}
@@ -214,26 +263,28 @@ def rank_program(g, core, T, topo):
     far_engines = topo.engines(core, dest[both[0]])
     share = len(far_engines) // 2
 
-    dma("Y", R("nbi"), T.nb[:])
-    dma("S", R("pathi", 0, 512), T.path0[:, 0:512])
-    dma("S", R("pathi", 512, V), T.path0[:, 512:V])
+    dma("S", R("pathi", 0, 512), T.path0[:, 0:512], late=1.9)
+    dma("Y", R("pathi", 512, V), T.path0[:, 512:V], late=2.4)
+    dma("Y", R("nbi"), T.nb[:], late=2.9)
     for k in range(8):
-        dma("Y", (T.X[:, k], "X", 0, 512), T.lk[k], grp="lk")
+        dma("YS"[k & 1], (T.X[:, k], "X", 64 * k, 64 * k + 64, 64), T.lk[k], late=4.0)
     for k in range(8):
-        dma("Y", (T.O[0:16, k], "O", 0, 512), T.org[k], grp="org")
+        last_load = dma("Y", (T.O[0:16, k], "O", 64 * k, 64 * k + 64, 64), T.org[k], late=4.5)
     for k, d in enumerate(order):
-        dma("Y", R("shi", 16 * k, 16 * k + 16), T.shown[:, 16 * d - 16:16 * d], grp="shown")
-    dma("Y", R("ati"), T.at0[:])
+        dma("Y", R("shi", 16 * k, 16 * k + 16), T.shown[:, 16 * d - 16:16 * d], after=[last_load])
+    dma("Y", R("ati"), T.at0[:], after=[last_load])
+    dma("Y", R("TL"), T.toll[:], after=[last_load])
 
     iota(R("SV"), [[-16, 8], [256, 2], [-2, 8]], 0, 1)
     iota(R("kci", 0, 1), [[0, 1]], 0, 1, flt=False)
     iota(R("DD"), [[-1, 128]], 0, 1)
     iota(R("RG"), [[1, 8], [0, 16]], 0, 0)
-    iota(R("NM0"), [[0, 2], [2, 512]], r * V + 1, 0)
     iota(R("RQ"), [[0, 8], [1, 16]], 0, 0)
+    iota(R("DN8"), [[1, 2], [32, 32]], 0, 0)
+    iota(R("slot"), [[16, 112]], 0, 0)
 
-    GC, QC, WA, WB, WC, KC, Q0, QN, C2, Q2 = [R("col", j, j + 1) for j in range(10)]
-    for n in ("MEQ", "MSG", "ZT", "DP0", "DP", "DN", "MPK"):
+    GC, QC, Q0, Q14, Q15, KC, QN, Q2, WE, WM, W1, W2, W3, WS, WC, WN = [R("col", j, j + 1) for j in range(16)]
+    for n in ("MEQ", "MM", "MNE", "ZT", "DP0", "DP", "DN", "MPK"):
         memset(R(n), 0.0)
     for k in range(4):
         ts(R("SHF", 128 * k, 128 * k + 128), R("SV"), 256.0 * (k & 1) + (k >> 1), ALU.is_equal)
@@ -242,226 +293,202 @@ def rank_program(g, core, T, topo):
     memset(R("ONE"), 1.0)
     copy(R("col", 0, 2), R("gqi", 0, 2))
     ts(R("IDb"), R("DD"), 0.0, ALU.is_equal)
-    ts(WA, QC, 0.0, ALU.is_equal, BIG + 32768.0, ALU.mult)
-    ts(WB, QC, 15.0, ALU.is_equal, 32768.0 - BIG, ALU.mult)
-    ts(KC, GC, -4096.0, ALU.mult, 4096.0 * 127, ALU.add)
     ts(Q0, QC, 0.0, ALU.is_equal)
-    ts(R("ZT", 1, 2), QC, 15.0, ALU.is_equal)
-    ts(R("BOS"), R("RG"), GC, ALU.is_equal, -8192.0, ALU.mult)
-    ts(WC, WA, WB, ALU.add, -32768.0, ALU.add)
-    ts(R("MEQ", 15, 143, 16), R("RG", 0, 128, 16), GC, ALU.is_equal, -BIG, ALU.mult)
-    copy(R("B0", V, V + 8), R("ZT"))
-    ts(R("MSG", 15, 143, 16), R("RG", 0, 128, 16), GC, ALU.is_equal, WC, ALU.mult)
-    copy(R("nbf"), R("nbi"))
-    for n, c in (("I20", float(1 << 20)), ("NEG", -BIG), ("I192", 192 * BIG), ("IDf", 1.0), ("DK", KC), ("I4", 4.0), ("I256", -256.0)):
-        act(R(n), R("IDb"), scale=c)
-    act(QN, Q0, scale=-16384.0, bias=16384.0)
+    ts(Q14, QC, 14.0, ALU.is_equal)
+    ts(Q15, QC, 15.0, ALU.is_equal)
+    ts(KC, GC, -4096.0, ALU.mult, 4096.0 * 7, ALU.add)
+    ts(WE, QC, 15.0, ALU.is_lt, -BIG, ALU.mult)
+    ts(WM, QC, 15.0, ALU.is_equal, 32768.0, ALU.mult)
+    act(W1, Q15, scale=-2.0, bias=1.0)
+    act(W2, Q0, scale=-257.0, bias=1.0)
+    act(W3, Q15, scale=255.0, bias=W2)
+    act(WS, Q14, scale=-1.0, bias=Q15)
+    ts(WC, Q15, 1e18, ALU.mult, 1e17, ALU.mult)
+    act(WN, Q15, scale=-1.0)
+    ts(QN, QC, 0.0, ALU.not_equal, 1e18, ALU.mult)
+    ts(QN, QN, 1e17, ALU.mult)
     act(Q2, QC, scale=2.0)
-    act(R("TT0"), R("NM0", 0, 512), scale=Q0, bias=QN)
+
+    def spread(out, w):
+        ts(out, R("RG", 0, 128, 16), GC, ALU.is_equal, w, ALU.mult)
+
+    spread(R("MEQ", 15, 143, 16), WE)
+    spread(R("MM", 15, 143, 16), WM)
+    spread(R("MNE", 15, 143, 16), -1.0)
+    spread(R("MPK", 15, 143, 16), Q0)
+    ts(R("ZT", 0, 1), Q15, -241.0, ALU.mult)
+    ts(R("ZT", 1, 2), Q14, 240.0, ALU.mult)
+    ts(R("ZT", 2, 3), Q15, 16.0, ALU.mult)
+    ts(R("BOS"), R("RG"), GC, ALU.is_equal, -8192.0, ALU.mult)
+    for n, c in (("D1", W1), ("D2", -255.0), ("D15", WN), ("I19", float(1 << 19)), ("N23", -float(1 << 23)), ("NEG", -BIG), ("I192", 192.0 * (1 << 23)),
+                 ("IDf", 1.0), ("DK", KC), ("I4", 4.0), ("I256", -256.0)):
+        act(R(n), R("IDb"), scale=c)
+    spread(R("D2", 15, 128, 16), W3)
+    for n in ("SHT", "SHU"):
+        ts(R(n), R("DD"), -1.0, ALU.is_equal)
+        spread(R(n, 0, 128, 16), WC)
+    spread(R("SHT", 15, 128, 16), WS)
     select(R("TMS"), R("BOS"), ALU.is_gt, 0.0)
     select(R("TMS"), R("TMS"), ALU.not_equal, -float(1 << 21))
-    iota(R("NM1"), [[0, 2], [2, 512]], r * V + 2, 0)
-    iota(R("DN8"), [[1, 2], [32, 32]], 0, 0)
-    iota(R("slot"), [[16, 112]], 0, 0)
-    iota(R("TP"), [[256, W]], 0, 0)
-    dma("G", R("TP", 0, V), T.toll[:, 0:V], add=True)
-    dma("G", R("TP", V, W), T.toll[:, V:W], add=True)
+    copy(R("B0", V, V + 16), R("ZT"))
+    copy(R("B1", 0, 16), R("ZT"))
+    for t in (1, 2, 3):
+        copy(R("B%d" % t, PRE[t] + W, PRE[t] + W + 16), R("ZT"))
+
+    for hf in range(2):
+        lo, hi = 512 * hf, 512 * hf + 512
+        copy(R("PF", lo, hi), R("pathi", lo, hi))
+        act(R("EN", lo, hi), R("PF", lo, hi), ACT.Exp, STEP, BASE, 1.3 if hf == 0 else 0.0)
+        ts(R("FLG", lo, hi), R("pathi", lo, hi), 0.0, ALU.is_equal)
+        mms([(R("ps%d" % hf), R("D2"), R("FLG", lo, hi), True, False)])
+        mms([(R("ps%d" % hf), R("D1"), R("EN", lo, hi), False, True)])
+        move(R("B0", lo, hi), R("ps%d" % hf), hf == 1)
+    for pi in range(2):
+        iota(R("NF%d" % pi), [[2, 512]], r * V + 1 + pi, 0)
+        act(R("NM%d" % pi), R("NF%d" % pi), ACT.Exp, STEP, BASE)
+        act(R("ps%d" % (6 + pi)), R("NM%d" % pi))
+        act(R("TT%d" % pi), R("NM%d" % pi), scale=Q0, bias=QN)
 
     def shuffle(out, pi, e, first):
-        for hh in range(2):
-            k = 2 * pi + hh
-            mm(out, R("SHF", 128 * k, 128 * k + 128), R("nbf", 2 * e + hh, 512, 4), first and hh == 0, hh == 1)
+        return [(out, R("SHF", 128 * (2 * pi + hh), 128 * (2 * pi + hh) + 128), R("nbf", 2 * e + hh, 512, 4), first and hh == 0, hh == 1) for hh in range(2)]
 
-    def lists(pi):
+    copy(R("nbf"), R("nbi"))
+    for pi in range(2):
+        b = "ps%d" % (2 + 2 * pi)
+        mms(shuffle(R(b, 0, 128), pi, 0, True) + shuffle(R(b, 128, 256), pi, 1, True))
         for e in range(2):
-            shuffle(R("ps%d" % (4 + 3 * pi), 128 * e, 128 * e + 128), pi, e, True)
+            ts(R("L0", 256 * pi + e, 256 * pi + 256, 2), R(b, 128 * e, 128 * e + 128), float(V), ALU.min)
+        for e in range(2):
+            copy(R("L", 256 * pi + e, 256 * pi + 256, 2), R(b, 128 * e, 128 * e + 128))
 
-    def lists_out(pi, name):
-        for e in range(2):
-            o, src = R(name, 256 * pi + e, 256 * pi + 256, 2), R("ps%d" % (4 + 3 * pi), 128 * e, 128 * e + 128)
-            if name == "L0":
-                ts(o, src, float(V), ALU.min)
-            else:
-                copy(o, src)
-
-    lists(0)
-    lists(1)
-    copy(R("B0", 0, 512), R("pathi", 0, 512))
-    lists_out(0, "L0")
-    copy(R("B0", 512, V), R("pathi", 512, V))
-
-    def link_prep():
-        for e in range(2):
-            copy(R("Xb", 256 * e, 256 * e + 256), R4("X", e))
-        act(R("DNb"), R("Xb"), scale=1.0 / 16, bias=192.0 - 15.0 / 32)
-        for e in range(2):
-            copy(R("Ob", 256 * e, 256 * e + 256, p1=16), R4("O", e, 16))
-        ts(R("R16", p1=16), R("RQ", p1=16), R("col", 1, 2, p1=16), ALU.is_equal, -256.0, ALU.mult)
+    for e in range(2):
+        copy(R("Xb", 256 * e, 256 * e + 256), R4("X", e))
+        copy(R("Ob", 256 * e, 256 * e + 256, p1=16), R4("O", e, 16))
+    act(R("DNb"), R("Xb"), scale=1.0 / 16, bias=192.0 - 15.0 / 32)
+    ts(R("R16", p1=16), R("RQ", p1=16), R("col", 1, 2, p1=16), ALU.is_equal, -256.0, ALU.mult)
 
     def link_tables(pi):
         for e in range(2):
-            o = R("ps5", 128 * e, 128 * e + 128)
+            o = R("ps3", 128 * e, 128 * e + 128)
             ob = R("Ob", 256 * e + pi, 256 * e + 256, 2, p1=16)
-            mm(o, R("Xb", 256 * e + pi, 256 * e + 256, 2), R("IDb"), True, False)
-            mm(o, ob, R("R16", p1=16), False, True)
-            mm(R("ps5", 256 + 16 * e, 272 + 16 * e), ob, R("IDb", 0, 16, p1=16), True, True)
+            mms([(o, R("Xb", 256 * e + pi, 256 * e + 256, 2), R("IDb"), True, False), (o, ob, R("R16", p1=16), False, True),
+                 (R("ps3", 256 + 16 * e, 272 + 16 * e), ob, R("IDb", 0, 16, p1=16), True, True)])
         for e in range(2):
-            o = R("ps6", 128 * e, 128 * e + 128)
-            mm(o, R("Xb", 256 * e + pi, 256 * e + 256, 2), R("I20"), True, False)
-            mm(o, R("DNb", 256 * e + pi, 256 * e + 256, 2), R("NEG"), False, False)
-            mm(o, R("ONE"), R("I192"), False, False)
-            mm(o, R("ONE"), R("DK"), False, False)
-            shuffle(o, pi, e, False)
-
-    def link_tables_out(pi):
+            o = R("ps5", 128 * e, 128 * e + 128)
+            mms([(o, R("Xb", 256 * e + pi, 256 * e + 256, 2), R("I19"), True, False), (o, R("DNb", 256 * e + pi, 256 * e + 256, 2), R("N23"), False, False),
+                 (o, R("ONE", 0, 128), R("I192"), False, False), (o, R("ONE", 0, 128), R("DK"), False, False)] + shuffle(o, pi, e, False))
         for e in range(2):
-            act(R("LK", 256 * pi + e, 256 * pi + 256, 2), R("ps5", 128 * e, 128 * e + 128))
-        for e in range(2):
-            act(R("CST", 256 * pi + e, 256 * pi + 256, 2), R("ps6", 128 * e, 128 * e + 128))
-        for e in range(2):
-            src = R("ps5", 256 + 16 * e, 272 + 16 * e)
+            act(R("LK", 256 * pi + e, 256 * pi + 256, 2), R("ps3", 128 * e, 128 * e + 128))
+            act(R("CST", 256 * pi + e, 256 * pi + 256, 2), R("ps5", 128 * e, 128 * e + 128))
+            src = R("ps3", 256 + 16 * e, 272 + 16 * e)
             if pi == 0:
-                act(R("DP0", e, 32, 2), src, bias=float(V))
-            act(R("DP", 64 * pi + e, 64 * pi + 32, 2), src, bias=float(W))
+                act(R("DP0", e, 32, 2), src, bias=float(V + 1))
+            act(R("DP", 64 * pi + e, 64 * pi + 32, 2), src, bias=float(W + 1))
+        for t in range(RO):
+            ts(R("DT%d" % t, 256 * pi, 256 * pi + 256), R("LK", 256 * pi, 256 * pi + 256), 16.0 * (t + 1), ALU.is_lt)
 
-    def down(t, pi):
-        ts(R("DT%d" % t, 256 * pi, 256 * pi + 256), R("LK", 256 * pi, 256 * pi + 256), 16.0 * (t + 1), ALU.is_lt, 1.0, ALU.add)
-
-    def path_constants():
-        ts(C2, Q0, R("ZT", 1, 2), ALU.add, 16384.0, ALU.mult)
-        ts(R("SHT"), R("DD"), -1.0, ALU.is_equal)
-        lists_out(1, "L0")
-        ts(R("SHT", 0, 128, 16), R("RG", 0, 128, 16), GC, ALU.is_equal, C2, ALU.mult)
-        lists_out(1, "L")
-
-    def crossing_constants():
-        copy(R("shu"), R("shi"))
-        memset(R("RST"), 1.0)
-        memset(R("C191"), 191.0 / 16)
-        memset(R("B1", 0, 8), 0.0)
-        memset(R("RST", 0, 112, 16), 0.0)
-        ts(R("SA0"), R("shi"), 8.0, ALU.add)
-
-    def more_constants():
-        for pi in range(2):
-            ts(R("DN", 64 * pi, 64 * pi + 32), R("DN8", 32 * pi, 32 * pi + 32), Q2, ALU.add)
-        ts(R("DN8"), R("DN8"), Q2, ALU.add, 8192.0, ALU.add)
-        act(R("SA1"), R("SA0"), bias=float(GH - 8))
-        act(R("slot"), R("slot"), bias=QC)
-        for t in (1, 2, 3):
-            act(R("B%d" % t, PRE[t] + W, PRE[t] + W + 8), R("ZT"))
-        copy(R("atu"), R("ati"))
-        ts(R("MPK", 15, 143, 16), R("RG", 0, 128, 16), GC, ALU.is_equal, Q0, ALU.mult)
+    link_tables(0)
+    link_tables(1)
+    copy(R("shu"), R("shi"))
+    memset(R("RST"), 1.0)
+    memset(R("C191"), 191.0 / 16)
+    memset(R("RST", 0, 112, 16), 0.0)
+    ts(R("SA0"), R("shi"), float(PRE[1]), ALU.add)
+    for pi in range(2):
+        ts(R("DN", 128 * pi, 128 * pi + 32), R("DN8", 32 * pi, 32 * pi + 32), Q2, ALU.add)
+    ts(R("DN8"), R("DN8"), Q2, ALU.add, 8192.0, ALU.add)
+    act(R("SA1"), R("SA0"), bias=float(GH - PRE[1]))
+    act(R("slot"), R("slot"), bias=QC)
+    copy(R("atu"), R("ati"))
+    for k in range(4):
+        iota(R("TP", 704 * k, 704 * k + 704), [[1024, 704]], 1024 * 704 * k, 0)
 
     def window(t):
-        return R("B%d" % t, PRE[t], PRE[t] + (V if t == 0 else W) + 8)
+        return R("B%d" % t, PRE[t], PRE[t] + (V if t == 0 else W) + 16)
 
-    def offsets(t, pi, c, lo=0, hi=64):
-        return R("L0" if t == 0 else "L", 256 * pi + 64 * c + lo, 256 * pi + 64 * c + hi)
-
-    def loops(t, pi, c, lo=0, hi=64):
-        tt(R("EQ", V * c + 16 * lo, V * c + 16 * hi), IND(window(t), offsets(t, pi, c, lo, hi)), R("NM%d" % pi, 16 * lo, 16 * hi), ALU.is_equal)
-
-    def filled(t, pi, c):
-        act(R("SG", V * c, V * c + V), IND(window(t), offsets(t, pi, c)), ACT.Sign)
-
-    def scores(t, pi, c, part="all", bank=0):
-        o = R("ps%d" % (bank + c), 0, 64)
-        lo = 256 * pi + 64 * c
-        if part != "close":
-            for q in range(16):
-                mm(o, R("MSG", 15 - q, 143 - q), R("SG", V * c + q, V * c + V, 16), q == 0, False)
-        if part == "all":
-            mm(o, R("NEG"), R("DT%d" % t, lo, lo + 64), False, False)
-        if part != "close":
-            for q in range(16):
-                mm(o, R("MEQ", 15 - q, 143 - q), R("EQ", V * c + q, V * c + V, 16), False, False)
-        if part == "close":
-            mm(o, R("NEG"), R("DT%d" % t, lo, lo + 64), False, False)
-        if part != "open":
-            mm(o, R("IDf"), R("CST", lo, lo + 64), False, True)
-
-    def running(t, pi, c, crit, bank=0):
-        base = 0 if crit else 256
-        if c == 0:
-            prev = R(("DP0" if t == 0 else "DP") if crit else "DN", 64 * pi, 64 * pi + 64)
+    def neighbour(t, pi, i, k, on_v, direct):
+        src = IND(window(t), R("L0" if t == 0 else "L", 256 * pi + 32 * i, 256 * pi + 32 * i + 32))
+        ga, eq = R("GA%d" % k, 512 * i, 512 * i + 512), R("EQ%d" % k, 512 * i, 512 * i + 512)
+        move(ga, src, on_v)
+        if direct:
+            tt(eq, src, R("NM%d" % pi), ALU.is_equal)
         else:
-            prev = R("RUN", base + 64 * c - 64, base + 64 * c)
-        tt(R("RUN", base + 64 * c, base + 64 * c + 64), R("ps%d" % (bank + c), 0, 64), prev, ALU.max)
+            tt(eq, ga, R("ps%d" % (6 + pi)), ALU.is_equal)
+
+    def scores(t, pi, i0, i1, k, o):
+        lo, hi = 256 * pi + 32 * i0, 256 * pi + 32 * i1
+        late = (t, pi) == (0, 0) and i1 < 7
+        if not late:
+            mms([(o, R("IDf"), R("CST", lo, hi), True, False), (o, R("NEG"), R("DT%d" % t, lo, hi), False, False)])
+        turn(o, "MM", "GA%d" % k, 512 * i0, 512 * i1, late, False)
+        turn(o, "MEQ", "EQ%d" % k, 512 * i0, 512 * i1, False, not late)
+        if late:
+            mms([(o, R("IDf"), R("CST", lo, hi), False, False), (o, R("NEG"), R("DT%d" % t, lo, hi), False, True)])
 
     def nh_list(t, pi):
         return R("NH", 64 * t + 32 * pi, 64 * t + 32 * pi + 32)
 
-    def winners(t, pi, crit, bank=0):
-        running(t, pi, 3, crit, bank)
-        base = 192 if crit else 448
-        k = 0 if crit else 32
-        tt(R("RI", k, k + 32), R("RUN", base, base + 32), R("RUN", base + 32, base + 64), ALU.max)
-        ts(R("RA", k, k + 32), R("RI", k, k + 32), 4095, ALU.bitwise_and)
-        copy(R("PL", 32 * t, 32 * t + 32) if crit else nh_list(t, pi), R("RA", k, k + 32))
-
-    def choice(t, pi, crit, early=0, done=0, fill=None):
-        for c in range(4):
-            if c >= done:
-                loops(t, pi, c)
-            if c >= early:
-                filled(t, pi, c)
-            if ("a", c) in fill:
-                fill[("a", c)]()
-            scores(t, pi, c)
-            if c == 3:
-                for k in range(3):
-                    running(t, pi, k, crit)
-            if c in fill:
-                fill[c]()
-        winners(t, pi, crit)
-
-    def first_choice():
-        loops(0, 0, 0)
-        filled(0, 0, 0)
-        link_prep()
-        scores(0, 0, 0, "open")
-        link_tables(0)
-        loops(0, 0, 1)
-        filled(0, 0, 1)
-        link_tables_out(0)
-        scores(0, 0, 1, "open")
-        loops(0, 0, 2)
-        filled(0, 0, 2)
-        down(0, 0)
-        scores(0, 0, 0, "close")
-        scores(0, 0, 1, "close")
-        scores(0, 0, 2)
-        loops(0, 0, 3)
-        filled(0, 0, 3)
-        scores(0, 0, 3)
-        carry(0, 1)
-        act(R("TT1"), R("NM1", 0, 512), scale=Q0, bias=QN)
-        path_constants()
-        for c in range(3):
-            running(0, 0, c, True)
-        winners(0, 0, True)
-        dma("Y", R("tg"), T.toll[:, V:W])
-        dma("Y", R("H", V, W), R("TP", V, W))
-
-    def crit_nh(t):
+    def advertisers(t):
         pi = t & 1
+        prev = R("DP0" if t == 0 else "DP", 64 * pi, 64 * pi + 64)
+        for c, (i0, i1) in enumerate(((0, 2), (2, 4), (4, 6), (6, 7), (7, 8))):
+            for i in range(i0, i1):
+                neighbour(t, pi, i, 0, i in CFG["crit_v"], i in CFG["direct"])
+            o = R("ps%d" % (c & 1), 0, 32 * (i1 - i0))
+            scores(t, pi, i0, i1, 0, o)
+            if c < 3:
+                tt(R("RUN", 64 * c, 64 * c + 64), o, prev, ALU.max)
+                prev = R("RUN", 64 * c, 64 * c + 64)
+            if c == 2:
+                tt(R("RUN", 192, 224), R("RUN", 128, 160), R("RUN", 160, 192), ALU.max)
+            if c == 3:
+                tt(R("RUN", 224, 256), o, R("RUN", 192, 224), ALU.max)
+            if c == 4:
+                tt(R("RI", 0, 32), o, R("RUN", 224, 256), ALU.max)
+        ts(R("RA", 0, 32), R("RI", 0, 32), 4095, ALU.bitwise_and)
+        copy(R("PL", 32 * t, 32 * t + 32), R("RA", 0, 32))
         tt(R("NI"), R("RI", 0, 32), R("DN8", 32 * pi, 32 * pi + 32), ALU.max)
         ts(R("NA"), R("NI"), 4095, ALU.bitwise_and)
         copy(nh_list(t, pi), R("NA"))
 
-    def path_gather(t, hf, on_v, bank=2):
-        out = R("PG", 256 * hf, 256 * hf + 256)
-        move(out, IND(window(t), R("PL", 32 * t + 16 * hf, 32 * t + 16 * hf + 16)), on_v)
-        mm(R("ps%d" % (bank + hf), 0, 256), R("SHT"), out, True, True)
+    def others(t):
+        pi, k = 1 - (t & 1), 1 + (t & 1)
+        for c in range(4):
+            for i in (2 * c, 2 * c + 1):
+                neighbour(t, pi, i, k, i in CFG["non_v"], i in CFG["direct"])
+            scores(t, pi, 2 * c, 2 * c + 2, k, R("ps2", 64 * c, 64 * c + 64))
+        tt(R("RUN2", 0, 128), R("ps2", 0, 128), R("DN", 128 * pi, 128 * pi + 128), ALU.max)
+        tt(R("RUN2", 128, 256), R("ps2", 128, 256), R("RUN2", 0, 128), ALU.max)
+        tt(R("RUN2", 256, 320), R("RUN2", 128, 192), R("RUN2", 192, 256), ALU.max)
+        tt(R("RI", 32, 64), R("RUN2", 256, 288), R("RUN2", 288, 320), ALU.max)
+        ts(R("RA", 32, 64), R("RI", 32, 64), 4095, ALU.bitwise_and)
+        copy(nh_list(t, pi), R("RA", 32, 64))
 
-    def path_store(t, hf, bank=2):
+    def advertise(t):
         pi = t & 1
-        lo = PRE[t + 1] + 512 * hf
-        tt(R("B%d" % (t + 1), lo + pi, lo + 512, 2), R("ps%d" % (bank + hf), 0, 256), R("TT%d" % pi, 256 * hf, 256 * hf + 256), ALU.min)
+        for hf in range(2):
+            pg, tt_ = R("PG", 256 * hf, 256 * hf + 256), R("TT%d" % pi, 256 * hf, 256 * hf + 256)
+            move(pg, IND(window(t), R("PL", 32 * t + 16 * hf, 32 * t + 16 * hf + 16)), hf == 1)
+            if t < RO - 1:
+                o = R("ps%d" % (3 * hf), 0, 256)
+                mms([(o, R("D15"), R("ONE"), True, False)])
+                mms([(o, R("SHT"), pg, False, True)])
+                lo = PRE[t + 1] + 512 * hf
+                tt(R("B%d" % (t + 1), lo + pi, lo + 512, 2), o, tt_, ALU.min)
+        if t >= RO - 2:
+            for hf in range(2):
+                lo, hi = 256 * hf, 256 * hf + 256
+                o = R("ps%d" % (3 if t < RO - 1 else 3 * hf), lo, hi)
+                mms([(o, R("SHU"), R("PG", lo, hi), True, True)])
+                tt(R("YE", lo, hi), o, R("TT%d" % pi, lo, hi), ALU.min)
+                act(R("YL", lo, hi), R("YE", lo, hi), ACT.Ln, math.exp(-(BASE + STEP * MID)), math.exp(-43.0), 1.5 if (t, hf) == (RO - 2, 0) else 0.0)
+                ts(R("YR", lo, hi), R("YL", lo, hi), 1.0 / STEP, ALU.mult, RND + MID, ALU.add)
+                act(R("YP", 2 * lo + pi, 2 * hi, 2), R("YR", lo, hi), ACT.Relu, bias=-RND)
+                if t == RO - 1:
+                    dma("Y", T.ypath[:, 2 * lo:2 * hi], R("YP", 2 * lo, 2 * hi))
 
     def carry(t, pi):
-        act(R("B%d" % (t + 1), PRE[t + 1] + pi, PRE[t + 1] + V, 2), R("B%d" % t, PRE[t] + pi, PRE[t] + V, 2))
+        copy(R("B%d" % (t + 1), PRE[t + 1] + pi, PRE[t + 1] + V, 2), R("B%d" % t, PRE[t] + pi, PRE[t] + V, 2))
 
     def masks(ch):
         out, k = {}, 0
@@ -474,190 +501,94 @@ def rank_program(g, core, T, topo):
             out[d] = sum(1 << e for e in es)
         return out
 
-    def last_buf(t):
-        return "SND" if t == 2 else "B%d" % (t + 2)
-
-    def span(j):
-        return 16 * order.index(chunks[j][0]), 16 * order.index(chunks[j][-1]) + 16
-
-    def differ(t, j, on_v=True):
-        m0, m1 = span(j)
-        b = "B%d" % (t + 1)
-        src = IND(R(b, PRE[t + 1], PRE[t + 1] + V), R("shu", m0, m1))
-        out = R("NE", 16 * m0, 16 * m1)
-        if t > 0:
-            tt(out, src, R(b, 16 * m0, 16 * m1), ALU.not_equal)
-        elif on_v:
-            ts(out, src, 0.0, ALU.not_equal)
-        else:
-            act(out, src, ACT.Sign)
-        for q in range(16):
-            mm(R("ps%d" % (6 + (j & 1)), 0, m1 - m0), R("MEQ", 15 - q, 143 - q), R("NE", 16 * m0 + q, 16 * m1, 16), q == 0, q == 15)
-
-    def count(t, j):
-        m0, m1 = span(j)
-        o, a, b = R("SC", m0, m1), R("RST", m0, m1), R("CH", m0, m1)
-        ts(b, R("ps%d" % (6 + (j & 1)), 0, m1 - m0), 0.0, ALU.is_lt, -1.0, ALU.mult)
-        add_op(pl, "V", lambda h: h.tensor_tensor_scan(o[0], a[0], b[0], 0.0, ALU.mult, ALU.subtract), [a, b], [o])
-        ps = R("ps%d" % (j & 1), 0, m1 - m0)
-        mm(ps, R("BOS"), R("C191", m0, m1), True, False)
-        mm(ps, R("TMS"), b, False, False)
-        mm(ps, R("BOS"), o, False, True)
-
-    def pick(t, j, split):
-        m0, m1 = span(j)
-        tt(R("M1", m0, m1), R("ps%d" % (j & 1), 0, m1 - m0), R("SA0" if t == 0 else "SA1", m0, m1), ALU.min)
-        if t == 0:
-            copy(R("XI", m0, m1), R("M1", m0, m1))
-        else:
-            tt(R("M2", m0, m1), R("M1", m0, m1), R("slot", m0, m1), ALU.max)
-            copy(R("XI", m0, m1), R("M2", m0, m1))
-        win = R("B%d" % (t + 1), 0, PRE[t + 1] + V)
-        mid = (m0 + m1) // 2 if split else m1
-        act(R(last_buf(t), 16 * m0, 16 * mid), IND(win, R("XI", m0, mid)))
-        if split:
-            copy(R(last_buf(t), 16 * mid, 16 * m1), IND(win, R("XI", mid, m1)))
-        mk = masks(chunks[j])
-        trs = []
-        for d in chunks[j]:
-            rid, pid, se = topo.addr(dest[d])
-            lo, at = PRE[t + 1] + V + G * (d - 1), G * order.index(d)
-            trs.append(RemoteDMATransfer(dst_ids=[DstId(rid=rid, pnc=pid)], dma_engine_mask=mk[d], remote_sem=T.sem["arr%d" % t],
-                                         src=T[last_buf(t)][:, at:at + G], dst=T["B%d" % (t + 1)][:, lo:lo + G]))
-        add_op(pl, "G", lambda h: h.remote_dma_fused(trs, local_sem=T.sem.sent), [R(last_buf(t), 16 * m0, 16 * m1)], [],
-               sem="sent", inc=share * len(trs))
-
     def crossing(t):
-        differ(t, 0)
-        differ(t, 1, on_v=t > 0)
-        if t == 0:
-            filled(0, 1, 0)
-        count(t, 0)
-        if t == 0:
-            differ(t, 2)
-        pick(t, 0, False)
-        if t > 0:
-            differ(t, 2)
-        count(t, 1)
-        pick(t, 1, False)
-        count(t, 2)
-        pick(t, 2, True)
-        add_op(pl, "X", None, [], [R("B%d" % (t + 1), PRE[t + 1] + V, PRE[t + 1] + W)], sem="arr%d" % t, inc=share * (N - 1))
-
-    def hop_table(t, pi, lo=0, hi=32, on_v=False):
-        k = 64 * t + 32 * pi
-        move(R("A" if t == 0 else "H", 32 * lo + pi, 32 * hi, 2), IND(R("TP"), R("NH", k + lo, k + hi)), on_v)
-
-    def follow(t):
-        for k in range(2):
-            if t == 1:
-                act(R("X1", k, V, 2), IND(R("H"), nh_list(0, k)))
+        b, last = "B%d" % (t + 1), "SND" if t == 2 else "B%d" % (t + 2)
+        sends = []
+        for j, ch in enumerate(chunks):
+            m0, m1 = 16 * order.index(ch[0]), 16 * order.index(ch[-1]) + 16
+            src = IND(R(b, PRE[t + 1], PRE[t + 1] + V), R("shu", m0, m1))
+            out = R("NE", 16 * m0, 16 * m1)
+            if t > 0:
+                tt(out, src, R(b, 16 * m0, 16 * m1), ALU.not_equal)
+            elif j != 1:
+                ts(out, src, 0.0, ALU.not_equal)
             else:
-                move(R("X2", 512 * k, 512 * k + 512), IND(R("H"), R("Q1", 32 * k, 32 * k + 32)), k == 0)
-
-    def follow_turn(t):
-        x = "X%d" % t
-        for q in range(16):
-            mm(R("ps5", 0, 64), R("MPK", 15 - q, 143 - q), R(x, q, V, 16), q == 0, q == 15)
-        dma("G", R("A"), R(x), add=True)
-
-    def follow_list(t):
-        copy(R("QI"), R("ps5", 0, 64))
-        ts(R("QA"), R("QI"), 8, ALU.arith_shift_right)
-        copy(R("Q%d" % t), R("QA"))
-
-    def ghost_floor():
-        act(R("FL"), R("tg"), scale=1.0 / 64, bias=192.0 - 63.0 / 128)
-
-    def ghost_sums():
-        for k in range(4):
-            lo = 448 * k
-            mm(R("ps%d" % (4 + k), 0, 448), R("I4"), R("tg", lo, lo + 448), True, False)
-            mm(R("ps%d" % (4 + k), 0, 448), R("I256"), R("FL", lo, lo + 448), False, True)
-
-    def ghost_sums_out():
-        for k in range(4):
-            act(R("FW", V + 448 * k, V + 448 * k + 448), R("ps%d" % (4 + k), 0, 448), bias=49152.0)
-
-    for t in range(RO - 1):
-        pi = t & 1
-        if t == 0:
-            first_choice()
-        else:
-            choice(t, pi, True, fill={3: lambda: loops(t, 1 - pi, 0, 0, 32)})
-        path_gather(t, 0, False)
-        path_gather(t, 1, True)
-        if t == 0:
-            crossing_constants()
-        else:
-            loops(t, 1 - pi, 0, 32, 64)
-        path_store(t, 0)
-        path_store(t, 1)
-        if t > 0:
-            filled(t, 1 - pi, 0)
-            filled(t, 1 - pi, 1)
-        crossing(t)
-        if t == 0:
-            link_tables(1)
-            link_tables_out(1)
-            more_constants()
-            lists_out(0, "L")
-            down(0, 1)
-        crit_nh(t)
-        down(t + 1, 1 - pi)
-        down(t + 1, pi)
-
-        def packets():
-            carry(t + 1, pi)
-            if t == 2:
-                hop_table(1, 0)
-                follow(1)
-            hop_table(t, pi)
+                act(out, src, ACT.Sign)
+            ps = R("ps%d" % (0 if j == 1 else 4), 0, m1 - m0)
+            turn(ps, "MNE" if t > 0 else "MEQ", "NE", 16 * m0, 16 * m1, True, True)
+            o, a, c = R("SC", m0, m1), R("RST", m0, m1), R("CH", m0, m1)
+            ts(c, ps, 0.0, ALU.is_lt, -1.0, ALU.mult)
+            add("V", lambda h, o=o, a=a, c=c: h.tensor_tensor_scan(o[0], a[0], c[0], 0.0, ALU.mult, ALU.subtract), [a, c], [o], 0.085)
+            ps = R("ps%d" % (1 if j == 1 else 5), 0, m1 - m0)
+            mms([(ps, R("BOS"), R("C191", m0, m1), True, False)])
+            mms([(ps, R("TMS"), c, False, False)])
+            mms([(ps, R("BOS"), o, False, True)])
+            tt(R("M1", m0, m1), ps, R("SA0" if t == 0 else "SA1", m0, m1), ALU.min)
             if t == 0:
-                ghost_floor()
-            if t == 1:
-                ghost_sums_out()
-
-        fill = {("a", 3): packets}
+                copy(R("XI", m0, m1), R("M1", m0, m1))
+            else:
+                tt(R("M2", m0, m1), R("M1", m0, m1), R("slot", m0, m1), ALU.max)
+                copy(R("XI", m0, m1), R("M2", m0, m1))
+            win = R(b, 0, PRE[t + 1] + V)
+            mid = (m0 + m1) // 2 if j == 2 else m1
+            act(R(last, 16 * m0, 16 * mid), IND(win, R("XI", m0, mid)))
+            if mid < m1:
+                copy(R(last, 16 * mid, 16 * m1), IND(win, R("XI", mid, m1)))
+            mk = masks(ch)
+            trs = []
+            for d in ch:
+                rid, pid, se = topo.addr(dest[d])
+                lo, at = PRE[t + 1] + V + G * (d - 1), G * order.index(d)
+                trs.append(RemoteDMATransfer(dst_ids=[DstId(rid=rid, pnc=pid)], dma_engine_mask=mk[d], remote_sem=T.sem["arr%d" % t],
+                                             src=T[last][:, at:at + G], dst=T[b][:, lo:lo + G]))
+            sends.append(add("G", lambda h, trs=trs: h.remote_dma_fused(trs, local_sem=T.sem.sent), [R(last, 16 * m0, 16 * m1)], [],
+                             0.6, CFG["fly"] + 0.6 * (2 - j), "sent", share * len(trs)))
+        landed = [add("X", None, [], [R(b, PRE[t + 1] + V, PRE[t + 1] + W)], 0.0, 0.0, "arr%d" % t, share * (N - 1), sends)]
+        if t == 0:
+            dma("G", R("TP", 0, V), T.toll[:, 0:V], True, after=landed)
+            dma("G", R("TP", V, W), T.toll[:, V:W], True, after=landed)
+            dma("Y", R("U2", V, W), R("TP", V, W))
         if t == 1:
-            fill[0] = ghost_sums
-        if t == 2:
-            fill[3] = lambda: follow_turn(1)
-        choice(t, 1 - pi, False, 1 if t == 0 else 2, 0 if t == 0 else 1, fill)
-        if t != 1:
-            hop_table(t, 1 - pi, on_v=True)
-    follow_list(1)
-    follow(2)
-    follow_turn(2)
+            dma("G", R("U2", V, W), T.toll[:, V:W], True, after=landed)
+            dma("Y", R("H", V, W), T.toll[:, V:W], after=landed)
 
-    for pi in (1, 0):
-        for c in range(4):
-            loops(3, pi, c)
-            filled(3, pi, c)
-            scores(3, pi, c, "all", 0 if pi else 4)
-            if pi == 1 and c == 3:
-                follow_list(2)
-            if pi == 0 and c == 1:
-                for k in range(3):
-                    running(3, 1, k, True)
-                winners(3, 1, True)
-                crit_nh(3)
-    path_gather(3, 0, False, 0)
-    path_gather(3, 1, False, 0)
-    hop_table(3, 1, on_v=True)
-    for k in range(3):
-        running(3, 0, k, False, 4)
-    winners(3, 0, False, 4)
-    hop_table(3, 0, 0, 16)
-    hop_table(3, 0, 16, 32, on_v=True)
-    tt(R("ZI"), IND(R("H"), R("Q2")), R("A"), ALU.add)
+    carry(0, 1)
+    for t in range(RO):
+        advertisers(t)
+        advertise(t)
+        if t < RO - 1:
+            crossing(t)
+        if t < RO - 2:
+            carry(t + 1, t & 1)
+        others(t)
+        if t == 0:
+            ts(R("FL"), R("TL", V, W), 1.0 / 64, ALU.mult, 192.0 - 63.0 / 128, ALU.add)
+            for k in range(4):
+                lo = 448 * k
+                mms([(R("ps2", 0, 448), R("I4"), R("TL", V + lo, V + lo + 448), True, False), (R("ps2", 0, 448), R("I256"), R("FL", lo, lo + 448), False, True)])
+                act(R("FW", V + lo, V + lo + 448), R("ps2", 0, 448), bias=49152.0)
+        if t == 2:
+            for pi in range(2):
+                tt(R("U2", pi, V, 2), IND(R("TP"), nh_list(2, pi)), R("TL", pi, V, 2), ALU.add)
+            for pi in range(2):
+                tt(R("U1", pi, V, 2), IND(R("U2"), nh_list(1, pi)), R("TL", pi, V, 2), ALU.add)
+            for pi in range(2):
+                act(R("T0", pi, V, 2), IND(R("U1"), nh_list(0, pi)))
+            turn(R("ps4", 0, 64), "MPK", "T0", 0, V, True, True)
+            copy(R("QI"), R("ps4", 0, 64))
+            ts(R("QA"), R("QI"), 10, ALU.arith_shift_right)
+            copy(R("Q"), R("QA"))
+
+    act(R("H", 1, V, 2), IND(R("TL"), nh_list(3, 1)))
     for hf in range(2):
-        path_store(3, hf, 0)
-        dma("Y", T.ypath[:, 512 * hf:512 * hf + 512], R("B4", 512 * hf, 512 * hf + 512))
-    ts(R("ZA"), R("ZI"), 255, ALU.bitwise_and)
-    copy(R("FW", 0, V), R("ZA"))
+        move(R("H", 512 * hf, 512 * hf + 512, 2), IND(R("TL"), R("NH", 192 + 16 * hf, 208 + 16 * hf)), hf == 1)
+    for hf in range(2):
+        lo, hi = 512 * hf, 512 * hf + 512
+        tt(R("ZI", lo, hi), IND(R("H"), R("Q", 32 * hf, 32 * hf + 32)), R("T0", lo, hi), ALU.add)
+        ts(R("ZA", lo, hi), R("ZI", lo, hi), 255, ALU.bitwise_and)
+        copy(R("FW", lo, hi), R("ZA", lo, hi))
     for k in range(4):
         lo = 512 * k
         move(R("YS", lo, lo + 512), IND(R("FW"), R("atu", 32 * k, 32 * k + 32)), k & 1 == 0)
         dma("Y", T.ysum[:, lo:lo + 512], R("YS", lo, lo + 512))
-    emit(pl, g, T)
+    emit(ops, g, T)

@@ -9,7 +9,18 @@ PRE = (0, 16, GH, GH)
 F32, BF, I32, U16 = "float32", "bfloat16", "int32", "uint16"
 STEP, BASE, MID = 0.00885, math.log(255.0), 3283
 RND = 12582912.0
-CFG = {"g": 1.3, "hop": 0.13, "fly": 4.0, "dma": 2.2, "pe": 0.00045, "crit_v": (0,), "non_v": (), "direct": ()}
+CYC = 0.00083
+
+ORDER = "000102050709030g0d0h0f0s040t06080a0u0v1f1g1c1h190i0e0c0b1i1k1l1j211s1n22231u1m163r2t0y0w0z151w1p1o35100x112g1213171q2s2z3b282u302n2b2629373c2c1a252f2v3o313m2w2x322y3d3q3p3e3n1d333450144z3u3s3v3t2a1x1v0m0p0l0n0o0j0k51523w1y3x53410r0q583y3z3h184w545b5559404o445a5g3k4q245642571b5i5f5n435c4x5d5j5e5h5k485r4y5o4t5l5s5p5q3f4p3l5m3i2h5t2l2m5u492p2o4s361t27384c1r605v4r4a5w2d2q4e2r4f5x5z2i4v2k4n6q61634h4j4m64654b62663j7h688g3967709t694d4i6z6a4g6b3g5y6c6d6e6f6g6h6l6m71727j7v7i7p736i746n7576776o786r7m8t6p6s797a6ta0906j6k6u6v6w7n7b6x7c6y81477k7l7o7s7t8d7q7r7w1e7x7u7y7z8084857d3a8283868p878q8s8r888u7f8x95948y8z8v91928w979c967e98997g9d9ab6b793899e8a9g9h9f8b2j9i8c202e8e8f9b4u9p9j9k1zae9l9n9m9o46459s8j8m9q9u8h8i9r9v9wb5ao9x9y8ka18l9zaaapaqa2aba3aca4ara5b8adasd5at8nafauagb9ahavaiawdmajaxc5cca7a68oakalazaya8ambda9babbb0bcbgbjbebfbhanb1bibpbkbmbn4kblbobsbtbrbq4lbubvb2bwc1bxetc9c3bycab3b4c2cdc4chcgbzcbc6c7cocec0c8cjckcfcpcicqcrclepcscmcteqcucnerd1eucvcwcxe0czcyesd4d0d2d6d3d7d8dieadjf2f8dkebdndwdld9dodpecdxeweeefdqedegdrdyeheve1dzeieye2ezddf0ejexdtdsekeldudve3f3e4f4e5emf1f5e7e6e8f6f7daf9fadefbfcene9fddffedbdgffdcfghdfyfhfifjfkeoflfmhgfvhah9fuheg5fxhchbfwg9hhg2fzhfhmgahsgihjhkg4g3g0g6g7hihlghhog1gdhngcg8gbhtfngkgjhufohpgehqhrglhvhwgfgmgggnfpdhhxgogpfqgshygthzgui0i4gqi1gri2i3gvi5i6frgxfsftgygwh3i7h4iai8ibgzh5h0i9ich6h1idihieh2h7ifijigh8ikii"
+FLIP = "252627282a2c2d2e2n34383q3w3x40414d505167686h6l6o6v797i8g8j8m9o9sa7akazb6bddtdye7ecelepfug9gvgwh9hgi6"
+
+
+def _numbers(s):
+    return [int(s[k:k + 2], 36) for k in range(0, len(s), 2)]
+
+
+CFG = {"g": 1.56, "hop": 0.13, "dma": 2.2, "pe": 0.00045, "blk": 0.8, "fix": 2.0, "wc": (1,), "wn": (1, 2, 3),
+       "order": _numbers(ORDER), "flip": set(_numbers(FLIP))}
 
 
 def _sb(n, dt):
@@ -25,7 +36,7 @@ SCRATCH = {
     "shi": _sb(112, I32), "shu": _sb(112, U16), "SA0": _sb(112, F32), "SA1": _sb(112, F32), "slot": _sb(112, F32),
     "ati": _sb(128, I32), "atu": _sb(128, U16),
     "kci": _sb(4, I32), "gqi": _sb(4, I32), "col": _sb(32, F32),
-    "SV": _sb(128, F32), "RG": _sb(128, F32), "DD": _sb(128, F32), "RQ": _sb(128, F32),
+    "SV": _sb(128, F32), "RG": _sb(128, F32), "RQ": _sb(128, F32),
     "SHF": _sb(512, F32), "IDb": _sb(128, BF), "IDf": _sb(128, F32), "NEG": _sb(128, BF), "I19": _sb(128, BF), "N23": _sb(128, BF),
     "DK": _sb(128, BF), "ONE": _sb(256, BF), "R16": _sb(128, BF), "I192": _sb(128, BF), "D1": _sb(128, BF), "D2": _sb(128, BF), "D15": _sb(128, BF),
     "MEQ": _sb(144, BF), "MM": _sb(144, BF), "MNE": _sb(144, BF), "MPK": _sb(144, F32), "SHT": _sb(128, BF), "SHU": _sb(128, BF),
@@ -35,8 +46,8 @@ SCRATCH = {
     "DT0": _sb(512, BF), "DT1": _sb(512, BF), "DT2": _sb(512, BF), "DT3": _sb(512, BF),
     "DP0": _sb(64, F32), "DP": _sb(128, F32), "DN": _sb(256, F32), "DN8": _sb(64, F32),
     "EQ0": _sb(4096, BF), "GA0": _sb(4096, BF), "EQ1": _sb(4096, BF), "GA1": _sb(4096, BF), "EQ2": _sb(4096, BF), "GA2": _sb(4096, BF),
-    "RUN": _sb(256, F32), "RUN2": _sb(384, F32),
-    "RI": _sb(64, I32), "RA": _sb(64, I32), "NI": _sb(32, I32), "NA": _sb(32, I32), "PL": _sb(128, U16), "NH": _sb(256, U16),
+    "RUN": _sb(384, F32), "RUN2": _sb(384, F32),
+    "RI": _sb(64, I32), "RA": _sb(64, I32), "NI": _sb(64, I32), "NA": _sb(64, I32), "PL": _sb(128, U16), "NH": _sb(256, U16),
     "PG": _sb(512, BF),
     "NE": _sb(GH, BF), "CH": _sb(112, BF), "SC": _sb(112, BF), "M1": _sb(112, F32), "M2": _sb(112, F32), "XI": _sb(112, U16),
     "TL": _sb(W, BF), "TP": _sb(W, F32), "U2": _sb(W, F32), "U1": _sb(V, F32), "T0": _sb(V, F32), "H": _sb(W, BF),
@@ -61,7 +72,7 @@ def depend(ops):
         deps = set(o["after"])
         for acc, wr in accs:
             for (m, b, bw) in touch.get(acc[1], []):
-                if overlap(acc, b) and (wr or bw or (acc[1].startswith("ps") and ops[m]["q"] != o["q"])):
+                if overlap(acc, b) and (wr or bw or (acc[1].startswith("ps") and (ops[m]["q"] != o["q"] or "alt" in o or "alt" in ops[m]))):
                     deps.add(m)
         for acc, wr in accs:
             touch.setdefault(acc[1], []).append((n, acc, wr))
@@ -69,13 +80,19 @@ def depend(ops):
 
 
 def arrange(ops):
+    order = CFG["order"]
+    if order and sorted(order) == list(range(len(ops))):
+        at = {n: k for k, n in enumerate(order)}
+        if all(at[m] < at[n] for n in order for m in ops[n]["deps"]):
+            return order
+    cost = [o["cost"] + o["gat"] * CFG["g"] * CYC + (0.03 if o["q"] in "VS" else 0.0) for o in ops]
     rank = [0.0] * len(ops)
     for n in range(len(ops) - 1, -1, -1):
-        rank[n] += ops[n]["cost"] + ops[n]["late"] + CFG["hop"]
+        rank[n] += cost[n] + ops[n]["late"] + CFG["hop"]
         for m in ops[n]["deps"]:
             rank[m] = max(rank[m], rank[n])
     taken = {}
-    for n in sorted(range(len(ops)), key=lambda k: (-1e9 if ops[k]["sem"] and not ops[k]["deps"] else -rank[k], k)):
+    for n in sorted(range(len(ops)), key=lambda k: (-1e9 if ops[k].get("first") or (ops[k]["sem"] and not ops[k]["deps"]) else -rank[k], k)):
         o = ops[n]
         t = 0.0
         for m in o["deps"]:
@@ -83,12 +100,14 @@ def arrange(ops):
             t = max(t, e["end"] + (0.0 if e["q"] == "P" and o["q"] == "P" else CFG["hop"]))
         spans = taken.setdefault(o["q"], [])
         k = 0
-        while k < len(spans) and (spans[k][1] <= t or spans[k][0] < t + o["cost"]):
+        while k < len(spans) and (spans[k][1] <= t or spans[k][0] < t + cost[n]):
             t = max(t, spans[k][1])
             k += 1
-        spans.insert(k, (t, t + o["cost"]))
-        o["start"], o["end"] = t, t + o["cost"] + o["late"]
-    return sorted(range(len(ops)), key=lambda k: (ops[k]["start"], k))
+        spans.insert(k, (t, t + cost[n]))
+        o["start"], o["end"] = t, t + cost[n] + o["late"]
+    CFG["ops"] = ops
+    CFG["first"] = sorted(range(len(ops)), key=lambda k: (ops[k]["start"], k))
+    return CFG["first"]
 
 
 def emit(ops, g, T):
@@ -159,7 +178,8 @@ def rank_program(g, core, T, topo):
     ndma = [0]
 
     def add(q, fn, reads, writes, cost, late=0.0, sem=None, inc=16, after=()):
-        ops.append({"q": q, "fn": fn, "r": reads, "w": writes, "cost": cost, "late": late, "sem": sem, "inc": inc, "after": after})
+        cost, gat = cost if isinstance(cost, tuple) else (cost, 0)
+        ops.append({"q": q, "fn": fn, "r": reads, "w": writes, "cost": cost, "gat": gat, "late": late, "sem": sem, "inc": inc, "after": after})
         return len(ops) - 1
 
     def R(name, lo=0, hi=None, step=1, p1=128):
@@ -186,12 +206,12 @@ def rank_program(g, core, T, topo):
     def val(a):
         return a[0] if isinstance(a, tuple) else a
 
-    def price(out, a, rate=1.0, fast=True):
+    def price(out, a, rate=1.0, fast=True, more=0.0):
         if len(a) == 6:
-            return 0.08 + a[4] * CFG["g"] * 0.00083
+            return (0.055, a[4])
         if fast and SCRATCH[out[1]][2] in (BF, U16) and SCRATCH[a[1]][2] in (BF, U16):
             rate = 0.5
-        return 0.03 + max(64, a[4] * rate) * 0.00083
+        return (max(64, a[4] * rate) * CYC + more, 0)
 
     def copy(out, in_):
         add("V", lambda h: h.tensor_copy(out[0], in_[0]), rd(in_), [out], price(out, in_))
@@ -215,13 +235,22 @@ def rank_program(g, core, T, topo):
             kw["scale"] = val(scale)
         if bias is not None:
             kw["bias"] = val(bias)
-        add("S", lambda h: h.activation(out[0], a[0], func, **kw), rd(a, scale, bias), [out], price(out, a, 1.0, False) + more)
+        add("S", lambda h: h.activation(out[0], a[0], func, **kw), rd(a, scale, bias), [out], price(out, a, 1.0, False, more))
+
+    def either(on_v, v_call, s_call):
+        v_call()
+        s_call()
+        s, v = ops.pop(), ops.pop()
+        if on_v != (len(ops) in CFG["flip"]):
+            s, v = v, s
+        s["alt"] = v
+        ops.append(s)
 
     def move(out, in_, on_v):
-        if on_v:
-            copy(out, in_)
-        else:
-            act(out, in_)
+        either(on_v, lambda: copy(out, in_), lambda: act(out, in_))
+
+    def affine(out, in_, scale, bias, on_v):
+        either(on_v, lambda: ts(out, in_, scale, ALU.mult, bias, ALU.add), lambda: act(out, in_, scale=scale, bias=bias))
 
     def mms(calls):
         def fn(h):
@@ -235,14 +264,14 @@ def rank_program(g, core, T, topo):
         mms([(out, R(sel, 15 - q, 143 - q), R(buf, lo + q, hi, 16), start and q == 0, stop and q == 15) for q in range(16)])
 
     def iota(out, pattern, base, cm, flt=True):
-        cost = 0.15 + out[4] * 0.00166
+        cost = 0.15 + out[4] * 2 * CYC
         if flt:
             add("G", lambda h: h.iota(out[0], pattern, base, cm, allow_small_or_imprecise_dtypes=True), [], [out], cost)
         else:
             add("G", lambda h: h.iota(out[0], pattern, base, cm), [], [out], cost)
 
-    def select(out, in_, op, fill):
-        add("G", lambda h: h.affine_select(out[0], in_[0], [[-1, 128]], op, fill, 0, 1), [in_], [out], 0.4)
+    def select(out, in_, op, fill, pattern=((-1, 128),), base=0, cm=1):
+        add("G", lambda h: h.affine_select(out[0], in_[0], [list(x) for x in pattern], op, fill, base, cm), [in_], [out], 0.19 + out[4] * 2 * CYC)
 
     def dma(q, out, in_, adding=False, late=None, after=()):
         s = "d%d" % ndma[0]
@@ -275,24 +304,30 @@ def rank_program(g, core, T, topo):
     dma("Y", R("ati"), T.at0[:], after=[last_load])
     dma("Y", R("TL"), T.toll[:], after=[last_load])
 
-    iota(R("SV"), [[-16, 8], [256, 2], [-2, 8]], 0, 1)
     iota(R("kci", 0, 1), [[0, 1]], 0, 1, flt=False)
-    iota(R("DD"), [[-1, 128]], 0, 1)
+    ops[-1]["first"] = True
+    iota(R("NF0"), [[2, 512]], r * V + 1, 0)
+    ops[-1]["first"] = True
+    memset(R("ONE"), 1.0)
+    memset(R("SV"), 1.0)
+    select(R("IDb"), R("ONE", 0, 128), ALU.is_equal, 0.0)
+    select(R("IDf"), R("SV"), ALU.is_equal, 0.0)
+    for k in range(4):
+        select(R("SHF", 128 * k, 128 * k + 128), R("SV"), ALU.is_equal, 0.0, ((-16, 8), (256, 2), (-2, 8)), -256 * (k & 1) - (k >> 1))
+    select(R("RST"), R("ONE", 0, 112), ALU.not_equal, 0.0, ((0, 7), (1, 16)), 0, 0)
+    for n in ("DP", "DN"):
+        iota(R(n), [[0, T[n].shape[1]]], 0, 0)
     iota(R("RG"), [[1, 8], [0, 16]], 0, 0)
     iota(R("RQ"), [[0, 8], [1, 16]], 0, 0)
     iota(R("DN8"), [[1, 2], [32, 32]], 0, 0)
     iota(R("slot"), [[16, 112]], 0, 0)
 
     GC, QC, Q0, Q14, Q15, KC, QN, Q2, WE, WM, W1, W2, W3, WS, WC, WN = [R("col", j, j + 1) for j in range(16)]
-    for n in ("MEQ", "MM", "MNE", "ZT", "DP0", "DP", "DN", "MPK"):
+    for n in ("MEQ", "MM", "MNE", "ZT", "DP0", "MPK"):
         memset(R(n), 0.0)
-    for k in range(4):
-        ts(R("SHF", 128 * k, 128 * k + 128), R("SV"), 256.0 * (k & 1) + (k >> 1), ALU.is_equal)
     ts(R("gqi", 0, 1), R("kci", 0, 1), 4, ALU.arith_shift_right)
     ts(R("gqi", 1, 2), R("kci", 0, 1), 15, ALU.bitwise_and)
-    memset(R("ONE"), 1.0)
     copy(R("col", 0, 2), R("gqi", 0, 2))
-    ts(R("IDb"), R("DD"), 0.0, ALU.is_equal)
     ts(Q0, QC, 0.0, ALU.is_equal)
     ts(Q14, QC, 14.0, ALU.is_equal)
     ts(Q15, QC, 15.0, ALU.is_equal)
@@ -321,33 +356,35 @@ def rank_program(g, core, T, topo):
     ts(R("ZT", 2, 3), Q15, 16.0, ALU.mult)
     ts(R("BOS"), R("RG"), GC, ALU.is_equal, -8192.0, ALU.mult)
     for n, c in (("D1", W1), ("D2", -255.0), ("D15", WN), ("I19", float(1 << 19)), ("N23", -float(1 << 23)), ("NEG", -BIG), ("I192", 192.0 * (1 << 23)),
-                 ("IDf", 1.0), ("DK", KC), ("I4", 4.0), ("I256", -256.0)):
-        act(R(n), R("IDb"), scale=c)
+                 ("DK", KC), ("I4", 4.0), ("I256", -256.0)):
+        affine(R(n), R("IDb"), c, 0.0, False)
     spread(R("D2", 15, 128, 16), W3)
     for n in ("SHT", "SHU"):
-        ts(R(n), R("DD"), -1.0, ALU.is_equal)
+        select(R(n), R("ONE", 0, 128), ALU.is_equal, 0.0, base=1)
         spread(R(n, 0, 128, 16), WC)
     spread(R("SHT", 15, 128, 16), WS)
     select(R("TMS"), R("BOS"), ALU.is_gt, 0.0)
     select(R("TMS"), R("TMS"), ALU.not_equal, -float(1 << 21))
-    copy(R("B0", V, V + 16), R("ZT"))
-    copy(R("B1", 0, 16), R("ZT"))
+    move(R("B0", V, V + 16), R("ZT"), True)
+    move(R("B1", 0, 16), R("ZT"), False)
     for t in (1, 2, 3):
-        copy(R("B%d" % t, PRE[t] + W, PRE[t] + W + 16), R("ZT"))
+        move(R("B%d" % t, PRE[t] + W, PRE[t] + W + 16), R("ZT"), False)
 
+    act(R("NM0"), R("NF0"), ACT.Exp, STEP, BASE, 1.3)
+    ops[-1]["first"] = True
     for hf in range(2):
         lo, hi = 512 * hf, 512 * hf + 512
         copy(R("PF", lo, hi), R("pathi", lo, hi))
-        act(R("EN", lo, hi), R("PF", lo, hi), ACT.Exp, STEP, BASE, 1.3 if hf == 0 else 0.0)
-        ts(R("FLG", lo, hi), R("pathi", lo, hi), 0.0, ALU.is_equal)
-        mms([(R("ps%d" % hf), R("D2"), R("FLG", lo, hi), True, False)])
-        mms([(R("ps%d" % hf), R("D1"), R("EN", lo, hi), False, True)])
+        act(R("EN", lo, hi), R("PF", lo, hi), ACT.Exp, STEP, BASE)
+        ts(R("FLG", lo, hi), R("EN", lo, hi), 255.0, ALU.is_equal)
+        mms([(R("ps%d" % hf), R("D1"), R("EN", lo, hi), True, False)])
+        mms([(R("ps%d" % hf), R("D2"), R("FLG", lo, hi), False, True)])
         move(R("B0", lo, hi), R("ps%d" % hf), hf == 1)
+    iota(R("NF1"), [[2, 512]], r * V + 2, 0)
+    act(R("NM1"), R("NF1"), ACT.Exp, STEP, BASE)
     for pi in range(2):
-        iota(R("NF%d" % pi), [[2, 512]], r * V + 1 + pi, 0)
-        act(R("NM%d" % pi), R("NF%d" % pi), ACT.Exp, STEP, BASE)
         act(R("ps%d" % (6 + pi)), R("NM%d" % pi))
-        act(R("TT%d" % pi), R("NM%d" % pi), scale=Q0, bias=QN)
+        affine(R("TT%d" % pi), R("NM%d" % pi), Q0, QN, True)
 
     def shuffle(out, pi, e, first):
         return [(out, R("SHF", 128 * (2 * pi + hh), 128 * (2 * pi + hh) + 128), R("nbf", 2 * e + hh, 512, 4), first and hh == 0, hh == 1) for hh in range(2)]
@@ -364,7 +401,7 @@ def rank_program(g, core, T, topo):
     for e in range(2):
         copy(R("Xb", 256 * e, 256 * e + 256), R4("X", e))
         copy(R("Ob", 256 * e, 256 * e + 256, p1=16), R4("O", e, 16))
-    act(R("DNb"), R("Xb"), scale=1.0 / 16, bias=192.0 - 15.0 / 32)
+    affine(R("DNb"), R("Xb"), 1.0 / 16, 192.0 - 15.0 / 32, False)
     ts(R("R16", p1=16), R("RQ", p1=16), R("col", 1, 2, p1=16), ALU.is_equal, -256.0, ALU.mult)
 
     def link_tables(pi):
@@ -378,8 +415,8 @@ def rank_program(g, core, T, topo):
             mms([(o, R("Xb", 256 * e + pi, 256 * e + 256, 2), R("I19"), True, False), (o, R("DNb", 256 * e + pi, 256 * e + 256, 2), R("N23"), False, False),
                  (o, R("ONE", 0, 128), R("I192"), False, False), (o, R("ONE", 0, 128), R("DK"), False, False)] + shuffle(o, pi, e, False))
         for e in range(2):
-            act(R("LK", 256 * pi + e, 256 * pi + 256, 2), R("ps3", 128 * e, 128 * e + 128))
-            act(R("CST", 256 * pi + e, 256 * pi + 256, 2), R("ps5", 128 * e, 128 * e + 128))
+            move(R("LK", 256 * pi + e, 256 * pi + 256, 2), R("ps3", 128 * e, 128 * e + 128), False)
+            move(R("CST", 256 * pi + e, 256 * pi + 256, 2), R("ps5", 128 * e, 128 * e + 128), False)
             src = R("ps3", 256 + 16 * e, 272 + 16 * e)
             if pi == 0:
                 act(R("DP0", e, 32, 2), src, bias=float(V + 1))
@@ -390,9 +427,7 @@ def rank_program(g, core, T, topo):
     link_tables(0)
     link_tables(1)
     copy(R("shu"), R("shi"))
-    memset(R("RST"), 1.0)
     memset(R("C191"), 191.0 / 16)
-    memset(R("RST", 0, 112, 16), 0.0)
     ts(R("SA0"), R("shi"), float(PRE[1]), ALU.add)
     for pi in range(2):
         ts(R("DN", 128 * pi, 128 * pi + 32), R("DN8", 32 * pi, 32 * pi + 32), Q2, ALU.add)
@@ -406,18 +441,16 @@ def rank_program(g, core, T, topo):
     def window(t):
         return R("B%d" % t, PRE[t], PRE[t] + (V if t == 0 else W) + 16)
 
-    def neighbour(t, pi, i, k, on_v, direct):
-        src = IND(window(t), R("L0" if t == 0 else "L", 256 * pi + 32 * i, 256 * pi + 32 * i + 32))
-        ga, eq = R("GA%d" % k, 512 * i, 512 * i + 512), R("EQ%d" % k, 512 * i, 512 * i + 512)
-        move(ga, src, on_v)
-        if direct:
-            tt(eq, src, R("NM%d" % pi), ALU.is_equal)
-        else:
-            tt(eq, ga, R("ps%d" % (6 + pi)), ALU.is_equal)
+    def neighbours(t, pi, c, k, on_v, whole):
+        for i, n in ((2 * c, 2),) if whole else ((2 * c, 1), (2 * c + 1, 1)):
+            src = IND(window(t), R("L0" if t == 0 else "L", 256 * pi + 32 * i, 256 * pi + 32 * (i + n)))
+            move(R("GA%d" % k, 512 * i, 512 * (i + n)), src, on_v and i == 2 * c)
+        for i in (2 * c, 2 * c + 1):
+            tt(R("EQ%d" % k, 512 * i, 512 * i + 512), R("GA%d" % k, 512 * i, 512 * i + 512), R("ps%d" % (6 + pi)), ALU.is_equal)
 
     def scores(t, pi, i0, i1, k, o):
         lo, hi = 256 * pi + 32 * i0, 256 * pi + 32 * i1
-        late = (t, pi) == (0, 0) and i1 < 7
+        late = (t, pi) == (0, 0) and i1 < 6
         if not late:
             mms([(o, R("IDf"), R("CST", lo, hi), True, False), (o, R("NEG"), R("DT%d" % t, lo, hi), False, False)])
         turn(o, "MM", "GA%d" % k, 512 * i0, 512 * i1, late, False)
@@ -431,38 +464,38 @@ def rank_program(g, core, T, topo):
     def advertisers(t):
         pi = t & 1
         prev = R("DP0" if t == 0 else "DP", 64 * pi, 64 * pi + 64)
-        for c, (i0, i1) in enumerate(((0, 2), (2, 4), (4, 6), (6, 7), (7, 8))):
-            for i in range(i0, i1):
-                neighbour(t, pi, i, 0, i in CFG["crit_v"], i in CFG["direct"])
-            o = R("ps%d" % (c & 1), 0, 32 * (i1 - i0))
-            scores(t, pi, i0, i1, 0, o)
-            if c < 3:
-                tt(R("RUN", 64 * c, 64 * c + 64), o, prev, ALU.max)
-                prev = R("RUN", 64 * c, 64 * c + 64)
-            if c == 2:
-                tt(R("RUN", 192, 224), R("RUN", 128, 160), R("RUN", 160, 192), ALU.max)
-            if c == 3:
-                tt(R("RUN", 224, 256), o, R("RUN", 192, 224), ALU.max)
-            if c == 4:
-                tt(R("RI", 0, 32), o, R("RUN", 224, 256), ALU.max)
+        for c in range(4):
+            neighbours(t, pi, c, 0, c == 0, c in CFG["wc"])
+            o = R("ps%d" % (c & 1), 0, 64)
+            scores(t, pi, 2 * c, 2 * c + 2, 0, o)
+            tt(R("RUN", 64 * c, 64 * c + 64), o, prev, ALU.max)
+            prev = R("RUN", 64 * c, 64 * c + 64)
+        tt(R("RI", 0, 32), R("RUN", 192, 224), R("RUN", 224, 256), ALU.max)
         ts(R("RA", 0, 32), R("RI", 0, 32), 4095, ALU.bitwise_and)
         copy(R("PL", 32 * t, 32 * t + 32), R("RA", 0, 32))
-        tt(R("NI"), R("RI", 0, 32), R("DN8", 32 * pi, 32 * pi + 32), ALU.max)
-        ts(R("NA"), R("NI"), 4095, ALU.bitwise_and)
-        copy(nh_list(t, pi), R("NA"))
+        if t == RO - 1:
+            tt(R("NI", 0, 32), R("RI", 0, 32), R("DN8", 32 * pi, 32 * pi + 32), ALU.max)
+            ts(R("NA", 0, 32), R("NI", 0, 32), 4095, ALU.bitwise_and)
+            copy(nh_list(t, pi), R("NA", 0, 32))
+        else:
+            tt(R("NI", 32 * pi, 32 * pi + 32), R("RI", 0, 32), R("DN8", 32 * pi, 32 * pi + 32), ALU.max)
 
     def others(t):
         pi, k = 1 - (t & 1), 1 + (t & 1)
         for c in range(4):
-            for i in (2 * c, 2 * c + 1):
-                neighbour(t, pi, i, k, i in CFG["non_v"], i in CFG["direct"])
+            neighbours(t, pi, c, k, c == 0, c in CFG["wn"])
             scores(t, pi, 2 * c, 2 * c + 2, k, R("ps2", 64 * c, 64 * c + 64))
         tt(R("RUN2", 0, 128), R("ps2", 0, 128), R("DN", 128 * pi, 128 * pi + 128), ALU.max)
         tt(R("RUN2", 128, 256), R("ps2", 128, 256), R("RUN2", 0, 128), ALU.max)
         tt(R("RUN2", 256, 320), R("RUN2", 128, 192), R("RUN2", 192, 256), ALU.max)
-        tt(R("RI", 32, 64), R("RUN2", 256, 288), R("RUN2", 288, 320), ALU.max)
-        ts(R("RA", 32, 64), R("RI", 32, 64), 4095, ALU.bitwise_and)
-        copy(nh_list(t, pi), R("RA", 32, 64))
+        if t == RO - 1:
+            tt(R("RI", 32, 64), R("RUN2", 256, 288), R("RUN2", 288, 320), ALU.max)
+            ts(R("RA", 32, 64), R("RI", 32, 64), 4095, ALU.bitwise_and)
+            copy(nh_list(t, pi), R("RA", 32, 64))
+        else:
+            tt(R("NI", 32 * pi, 32 * pi + 32), R("RUN2", 256, 288), R("RUN2", 288, 320), ALU.max)
+            ts(R("NA"), R("NI"), 4095, ALU.bitwise_and)
+            copy(R("NH", 64 * t, 64 * t + 64), R("NA"))
 
     def advertise(t):
         pi = t & 1
@@ -482,13 +515,14 @@ def rank_program(g, core, T, topo):
                 mms([(o, R("SHU"), R("PG", lo, hi), True, True)])
                 tt(R("YE", lo, hi), o, R("TT%d" % pi, lo, hi), ALU.min)
                 act(R("YL", lo, hi), R("YE", lo, hi), ACT.Ln, math.exp(-(BASE + STEP * MID)), math.exp(-43.0), 1.5 if (t, hf) == (RO - 2, 0) else 0.0)
-                ts(R("YR", lo, hi), R("YL", lo, hi), 1.0 / STEP, ALU.mult, RND + MID, ALU.add)
-                act(R("YP", 2 * lo + pi, 2 * hi, 2), R("YR", lo, hi), ACT.Relu, bias=-RND)
+                affine(R("YR", lo, hi), R("YL", lo, hi), 1.0 / STEP, RND + MID, False)
+                yp = R("YP", 2 * lo + pi, 2 * hi, 2)
+                either(False, lambda: ts(yp, R("YR", lo, hi), RND, ALU.max, RND, ALU.subtract), lambda: act(yp, R("YR", lo, hi), ACT.Relu, bias=-RND))
                 if t == RO - 1:
                     dma("Y", T.ypath[:, 2 * lo:2 * hi], R("YP", 2 * lo, 2 * hi))
 
     def carry(t, pi):
-        copy(R("B%d" % (t + 1), PRE[t + 1] + pi, PRE[t + 1] + V, 2), R("B%d" % t, PRE[t] + pi, PRE[t] + V, 2))
+        select(R("B%d" % (t + 1), PRE[t + 1] + pi, PRE[t + 1] + V, 2), R("B%d" % t, PRE[t] + pi, PRE[t] + V, 2), ALU.is_ge, 0.0, ((0, 512),), 0, 0)
 
     def masks(ch):
         out, k = {}, 0
@@ -506,20 +540,20 @@ def rank_program(g, core, T, topo):
         sends = []
         for j, ch in enumerate(chunks):
             m0, m1 = 16 * order.index(ch[0]), 16 * order.index(ch[-1]) + 16
-            src = IND(R(b, PRE[t + 1], PRE[t + 1] + V), R("shu", m0, m1))
-            out = R("NE", 16 * m0, 16 * m1)
-            if t > 0:
-                tt(out, src, R(b, 16 * m0, 16 * m1), ALU.not_equal)
-            elif j != 1:
-                ts(out, src, 0.0, ALU.not_equal)
-            else:
-                act(out, src, ACT.Sign)
-            ps = R("ps%d" % (0 if j == 1 else 4), 0, m1 - m0)
+            mid = ((m0 + m1) // 4) * 2
+            for n0, n1 in ((m0, m1),) if t > 0 else ((m0, mid), (mid, m1)):
+                src = IND(R(b, PRE[t + 1], PRE[t + 1] + V), R("shu", n0, n1))
+                out = R("NE", 16 * n0, 16 * n1)
+                if t > 0:
+                    tt(out, src, R(b, 16 * n0, 16 * n1), ALU.not_equal)
+                else:
+                    either(n0 == m0, lambda: ts(out, src, 0.0, ALU.not_equal), lambda: act(out, src, ACT.Sign))
+            ps = R("ps%d" % (0 if j & 1 else 4), 0, m1 - m0)
             turn(ps, "MNE" if t > 0 else "MEQ", "NE", 16 * m0, 16 * m1, True, True)
             o, a, c = R("SC", m0, m1), R("RST", m0, m1), R("CH", m0, m1)
-            ts(c, ps, 0.0, ALU.is_lt, -1.0, ALU.mult)
-            add("V", lambda h, o=o, a=a, c=c: h.tensor_tensor_scan(o[0], a[0], c[0], 0.0, ALU.mult, ALU.subtract), [a, c], [o], 0.085)
-            ps = R("ps%d" % (1 if j == 1 else 5), 0, m1 - m0)
+            either(False, lambda: ts(c, ps, 0.0, ALU.is_lt, -1.0, ALU.mult), lambda: act(c, ps, ACT.Sign))
+            add("V", lambda h, o=o, a=a, c=c: h.tensor_tensor_scan(o[0], a[0], c[0], 0.0, ALU.mult, ALU.subtract), [a, c], [o], 0.055)
+            ps = R("ps%d" % (1 if j & 1 else 5), 0, m1 - m0)
             mms([(ps, R("BOS"), R("C191", m0, m1), True, False)])
             mms([(ps, R("TMS"), c, False, False)])
             mms([(ps, R("BOS"), o, False, True)])
@@ -530,10 +564,8 @@ def rank_program(g, core, T, topo):
                 tt(R("M2", m0, m1), R("M1", m0, m1), R("slot", m0, m1), ALU.max)
                 copy(R("XI", m0, m1), R("M2", m0, m1))
             win = R(b, 0, PRE[t + 1] + V)
-            mid = (m0 + m1) // 2 if j == 2 else m1
-            act(R(last, 16 * m0, 16 * mid), IND(win, R("XI", m0, mid)))
-            if mid < m1:
-                copy(R(last, 16 * mid, 16 * m1), IND(win, R("XI", mid, m1)))
+            move(R(last, 16 * m0, 16 * mid), IND(win, R("XI", m0, mid)), False)
+            move(R(last, 16 * mid, 16 * m1), IND(win, R("XI", mid, m1)), True)
             mk = masks(ch)
             trs = []
             for d in ch:
@@ -541,8 +573,9 @@ def rank_program(g, core, T, topo):
                 lo, at = PRE[t + 1] + V + G * (d - 1), G * order.index(d)
                 trs.append(RemoteDMATransfer(dst_ids=[DstId(rid=rid, pnc=pid)], dma_engine_mask=mk[d], remote_sem=T.sem["arr%d" % t],
                                              src=T[last][:, at:at + G], dst=T[b][:, lo:lo + G]))
-            sends.append(add("G", lambda h, trs=trs: h.remote_dma_fused(trs, local_sem=T.sem.sent), [R(last, 16 * m0, 16 * m1)], [],
-                             0.6, CFG["fly"] + 0.6 * (2 - j), "sent", share * len(trs)))
+            n = add("G", lambda h, trs=trs: h.remote_dma_fused(trs, local_sem=T.sem.sent), [R(last, 16 * m0, 16 * m1)], [],
+                    0.6, 0.0, "sent", share * len(trs))
+            sends.append(add("X", None, [], [], CFG["blk"] * len([d for d in ch if d not in near]), CFG["fix"], None, 0, [n]))
         landed = [add("X", None, [], [R(b, PRE[t + 1] + V, PRE[t + 1] + W)], 0.0, 0.0, "arr%d" % t, share * (N - 1), sends)]
         if t == 0:
             dma("G", R("TP", 0, V), T.toll[:, 0:V], True, after=landed)
@@ -562,24 +595,24 @@ def rank_program(g, core, T, topo):
             carry(t + 1, t & 1)
         others(t)
         if t == 0:
-            ts(R("FL"), R("TL", V, W), 1.0 / 64, ALU.mult, 192.0 - 63.0 / 128, ALU.add)
             for k in range(4):
                 lo = 448 * k
+                affine(R("FL", lo, lo + 448), R("TL", V + lo, V + lo + 448), 1.0 / 64, 192.0 - 63.0 / 128, True)
                 mms([(R("ps2", 0, 448), R("I4"), R("TL", V + lo, V + lo + 448), True, False), (R("ps2", 0, 448), R("I256"), R("FL", lo, lo + 448), False, True)])
-                act(R("FW", V + lo, V + lo + 448), R("ps2", 0, 448), bias=49152.0)
+                affine(R("FW", V + lo, V + lo + 448), R("ps2", 0, 448), 1.0, 49152.0, False)
         if t == 2:
             for pi in range(2):
                 tt(R("U2", pi, V, 2), IND(R("TP"), nh_list(2, pi)), R("TL", pi, V, 2), ALU.add)
             for pi in range(2):
                 tt(R("U1", pi, V, 2), IND(R("U2"), nh_list(1, pi)), R("TL", pi, V, 2), ALU.add)
             for pi in range(2):
-                act(R("T0", pi, V, 2), IND(R("U1"), nh_list(0, pi)))
+                move(R("T0", pi, V, 2), IND(R("U1"), nh_list(0, pi)), False)
             turn(R("ps4", 0, 64), "MPK", "T0", 0, V, True, True)
             copy(R("QI"), R("ps4", 0, 64))
             ts(R("QA"), R("QI"), 10, ALU.arith_shift_right)
             copy(R("Q"), R("QA"))
 
-    act(R("H", 1, V, 2), IND(R("TL"), nh_list(3, 1)))
+    move(R("H", 1, V, 2), IND(R("TL"), nh_list(3, 1)), False)
     for hf in range(2):
         move(R("H", 512 * hf, 512 * hf + 512, 2), IND(R("TL"), R("NH", 192 + 16 * hf, 208 + 16 * hf)), hf == 1)
     for hf in range(2):

import math
from concourse.bass import DstId, RemoteDMATransfer
from concourse.mybir import AluOpType as ALU, ActivationFunctionType as ACT

N, V, G, W, P, RO = 8, 1024, 256, 2816, 2048, 4
GH = W - V
BIG = float(1 << 24)
PRE = (0, 16, GH, GH)
F32, BF, I32, U16 = "float32", "bfloat16", "int32", "uint16"
STEP, BASE, MID = 0.00885, math.log(255.0), 3283
RND = 12582912.0
CYC = 0.00083

ORDER = "000102050709030g0d0h0f0s040t06080a0u0v1f1g1c1h190i0e0c0b1i1k1l1j211s1n22231u1m163r2t0y0w0z151w1p1o35100x112g1213171q2s2z3b282u302n2b2629373c2c1a252f2v3o313m2w2x322y3d3q3p3e3n1d333450144z3u3s3v3t2a1x1v0m0p0l0n0o0j0k51523w1y3x53410r0q583y3z3h184w545b5559404o445a5g3k4q245642571b5i5f5n435c4x5d5j5e5h5k485r4y5o4t5l5s5p5q3f4p3l5m3i2h5t2l2m5u492p2o4s361t27384c1r605v4r4a5w2d2q4e2r4f5x5z2i4v2k4n6q61634h4j4m64654b62663j7h688g3967709t694d4i6z6a4g6b3g5y6c6d6e6f6g6h6l6m71727j7v7i7p736i746n7576776o786r7m8t6p6s797a6ta0906j6k6u6v6w7n7b6x7c6y81477k7l7o7s7t8d7q7r7w1e7x7u7y7z8084857d3a8283868p878q8s8r888u7f8x95948y8z8v91928w979c967e98997g9d9ab6b793899e8a9g9h9f8b2j9i8c202e8e8f9b4u9p9j9k1zae9l9n9m9o46459s8j8m9q9u8h8i9r9v9wb5ao9x9y8ka18l9zaaapaqa2aba3aca4ara5b8adasd5at8nafauagb9ahavaiawdmajaxc5cca7a68oakalazaya8ambda9babbb0bcbgbjbebfbhanb1bibpbkbmbn4kblbobsbtbrbq4lbubvb2bwc1bxetc9c3bycab3b4c2cdc4chcgbzcbc6c7cocec0c8cjckcfcpcicqcrclepcscmcteqcucnerd1eucvcwcxe0czcyesd4d0d2d6d3d7d8dieadjf2f8dkebdndwdld9dodpecdxeweeefdqedegdrdyeheve1dzeieye2ezddf0ejexdtdsekeldudve3f3e4f4e5emf1f5e7e6e8f6f7daf9fadefbfcene9fddffedbdgffdcfghdfyfhfifjfkeoflfmhgfvhah9fuheg5fxhchbfwg9hhg2fzhfhmgahsgihjhkg4g3g0g6g7hihlghhog1gdhngcg8gbhtfngkgjhufohpgehqhrglhvhwgfgmgggnfpdhhxgogpfqgshygthzgui0i4gqi1gri2i3gvi5i6frgxfsftgygwh3i7h4iai8ibgzh5h0i9ich6h1idihieh2h7ifijigh8ikii"
FLIP = "252627282a2c2d2e2n34383q3w3x40414d505167686h6l6o6v797i8g8j8m9o9sa7akazb6bddtdye7ecelepfug9gvgwh9hgi6"


def _numbers(s):
    return [int(s[k:k + 2], 36) for k in range(0, len(s), 2)]


CFG = {"g": 1.56, "hop": 0.13, "dma": 2.2, "pe": 0.00045, "blk": 0.8, "fix": 2.0, "wc": (1,), "wn": (1, 2, 3),
       "order": _numbers(ORDER), "flip": set(_numbers(FLIP))}


def _sb(n, dt):
    return ("sbuf", [128, n], dt)


SCRATCH = {
    "B0": _sb(V + 16, BF), "B1": _sb(16 + W + 16, BF), "B2": _sb(GH + W + 16, BF), "B3": _sb(GH + W + 16, BF),
    "SND": _sb(GH, BF), "YP": _sb(V, F32), "YE": _sb(512, BF), "YL": _sb(512, F32), "YR": _sb(512, F32),
    "pathi": _sb(V, I32), "PF": _sb(V, F32), "FLG": _sb(V, BF), "EN": _sb(V, BF), "nbi": _sb(512, I32), "nbf": _sb(512, F32),
    "X": ("sbuf", [128, 8, 2, 32], I32), "O": ("sbuf", [128, 8, 2, 32], I32),
    "Xb": _sb(512, BF), "DNb": _sb(512, BF), "Ob": _sb(512, BF),
    "shi": _sb(112, I32), "shu": _sb(112, U16), "SA0": _sb(112, F32), "SA1": _sb(112, F32), "slot": _sb(112, F32),
    "ati": _sb(128, I32), "atu": _sb(128, U16),
    "kci": _sb(4, I32), "gqi": _sb(4, I32), "col": _sb(32, F32),
    "SV": _sb(128, F32), "RG": _sb(128, F32), "RQ": _sb(128, F32),
    "SHF": _sb(512, F32), "IDb": _sb(128, BF), "IDf": _sb(128, F32), "NEG": _sb(128, BF), "I19": _sb(128, BF), "N23": _sb(128, BF),
    "DK": _sb(128, BF), "ONE": _sb(256, BF), "R16": _sb(128, BF), "I192": _sb(128, BF), "D1": _sb(128, BF), "D2": _sb(128, BF), "D15": _sb(128, BF),
    "MEQ": _sb(144, BF), "MM": _sb(144, BF), "MNE": _sb(144, BF), "MPK": _sb(144, F32), "SHT": _sb(128, BF), "SHU": _sb(128, BF),
    "BOS": _sb(128, BF), "TMS": _sb(128, BF), "C191": _sb(112, BF), "RST": _sb(112, BF),
    "NF0": _sb(512, F32), "NF1": _sb(512, F32), "NM0": _sb(512, BF), "NM1": _sb(512, BF), "TT0": _sb(512, BF), "TT1": _sb(512, BF), "ZT": _sb(16, BF),
    "L0": _sb(512, U16), "L": _sb(512, U16), "CST": _sb(512, F32), "LK": _sb(512, BF),
    "DT0": _sb(512, BF), "DT1": _sb(512, BF), "DT2": _sb(512, BF), "DT3": _sb(512, BF),
    "DP0": _sb(64, F32), "DP": _sb(128, F32), "DN": _sb(256, F32), "DN8": _sb(64, F32),
    "EQ0": _sb(4096, BF), "GA0": _sb(4096, BF), "EQ1": _sb(4096, BF), "GA1": _sb(4096, BF), "EQ2": _sb(4096, BF), "GA2": _sb(4096, BF),
    "RUN": _sb(384, F32), "RUN2": _sb(384, F32),
    "RI": _sb(64, I32), "RA": _sb(64, I32), "NI": _sb(64, I32), "NA": _sb(64, I32), "PL": _sb(128, U16), "NH": _sb(256, U16),
    "PG": _sb(512, BF),
    "NE": _sb(GH, BF), "CH": _sb(112, BF), "SC": _sb(112, BF), "M1": _sb(112, F32), "M2": _sb(112, F32), "XI": _sb(112, U16),
    "TL": _sb(W, BF), "TP": _sb(W, F32), "U2": _sb(W, F32), "U1": _sb(V, F32), "T0": _sb(V, F32), "H": _sb(W, BF),
    "QI": _sb(64, I32), "QA": _sb(64, I32), "Q": _sb(64, U16),
    "FL": _sb(GH, BF), "I4": _sb(128, BF), "I256": _sb(128, BF), "FW": _sb(W, BF),
    "ZI": _sb(V, I32), "ZA": _sb(V, I32), "YS": _sb(P, BF),
}
for _b in range(8):
    SCRATCH["ps%d" % _b] = ("psum", [128, 512], F32)

SEMAPHORES = ["qV", "qS", "qP", "qG", "sent", "arr0", "arr1", "arr2"] + ["d%d" % _b for _b in range(60)]


def overlap(a, b):
    return a[1].startswith("ps") or (a[2] < b[3] and b[2] < a[3])


def depend(ops):
    touch = {}
    for n, o in enumerate(ops):
        accs = [(a, False) for a in o["r"]] + [(a, True) for a in o["w"]]
        deps = set(o["after"])
        for acc, wr in accs:
            for (m, b, bw) in touch.get(acc[1], []):
                if overlap(acc, b) and (wr or bw or (acc[1].startswith("ps") and (ops[m]["q"] != o["q"] or "alt" in o or "alt" in ops[m]))):
                    deps.add(m)
        for acc, wr in accs:
            touch.setdefault(acc[1], []).append((n, acc, wr))
        o["deps"] = deps


def arrange(ops):
    order = CFG["order"]
    if order and sorted(order) == list(range(len(ops))):
        at = {n: k for k, n in enumerate(order)}
        if all(at[m] < at[n] for n in order for m in ops[n]["deps"]):
            return order
    cost = [o["cost"] + o["gat"] * CFG["g"] * CYC + (0.03 if o["q"] in "VS" else 0.0) for o in ops]
    rank = [0.0] * len(ops)
    for n in range(len(ops) - 1, -1, -1):
        rank[n] += cost[n] + ops[n]["late"] + CFG["hop"]
        for m in ops[n]["deps"]:
            rank[m] = max(rank[m], rank[n])
    taken = {}
    for n in sorted(range(len(ops)), key=lambda k: (-1e9 if ops[k].get("first") or (ops[k]["sem"] and not ops[k]["deps"]) else -rank[k], k)):
        o = ops[n]
        t = 0.0
        for m in o["deps"]:
            e = ops[m]
            t = max(t, e["end"] + (0.0 if e["q"] == "P" and o["q"] == "P" else CFG["hop"]))
        spans = taken.setdefault(o["q"], [])
        k = 0
        while k < len(spans) and (spans[k][1] <= t or spans[k][0] < t + cost[n]):
            t = max(t, spans[k][1])
            k += 1
        spans.insert(k, (t, t + cost[n]))
        o["start"], o["end"] = t, t + cost[n] + o["late"]
    CFG["ops"] = ops
    CFG["first"] = sorted(range(len(ops)), key=lambda k: (ops[k]["start"], k))
    return CFG["first"]


def emit(ops, g, T):
    depend(ops)
    order = arrange(ops)
    queues = {"V": g.vector, "S": g.scalar, "P": g.tensor, "G": g, "Y": g.sync}
    total = {}
    for k, n in enumerate(order):
        o = ops[n]
        o["at"] = k
        o["key"] = o["sem"] if o["sem"] is not None else "q" + o["q"]
        if o["sem"] is not None:
            total[o["sem"]] = total.get(o["sem"], 0) + o["inc"]
    known = {q: {} for q in queues}
    for n in order:
        o = ops[n]
        o["waits"] = []
        if o["q"] == "X":
            o["vc"] = {o["key"]: o["at"]}
            continue
        kn = known[o["q"]]
        for m in sorted(o["deps"], key=lambda k: -ops[k]["at"]):
            e = ops[m]
            if (e["q"] == "P" and o["q"] == "P") or kn.get(e["key"], -1) >= e["at"]:
                continue
            o["waits"].append(m)
            e["need"] = True
            for k, val in e["vc"].items():
                if kn.get(k, -1) < val:
                    kn[k] = val
        o["vc"] = dict(kn)
        o["vc"][o["key"]] = o["at"]
    count = {}
    for n in order:
        o = ops[n]
        if o["sem"] is None and o.get("need"):
            count[o["key"]] = count.get(o["key"], 0) + 1
            o["val"] = count[o["key"]]
    waited = set()
    for n in order:
        o = ops[n]
        if o["q"] == "X":
            continue
        h = queues[o["q"]]
        for m in o["waits"]:
            e = ops[m]
            if e["sem"] is None:
                h.wait_ge(T.sem[e["key"]], e["val"])
            else:
                h.wait_ge(T.sem[e["sem"]], total[e["sem"]])
                waited.add(e["sem"])
        ins = o["fn"](h)
        if o["sem"] is not None:
            if o["sem"] != "sent":
                ins.then_inc(T.sem[o["sem"]], o["inc"])
        elif o.get("need"):
            ins.then_inc(T.sem[o["key"]], 1)
    for s in total:
        if s not in waited:
            g.wait_ge(T.sem[s], total[s])


def rank_program(g, core, T, topo):
    r = T.rank_of(core)
    if r is None:
        return
    ops = []
    ndma = [0]

    def add(q, fn, reads, writes, cost, late=0.0, sem=None, inc=16, after=()):
        cost, gat = cost if isinstance(cost, tuple) else (cost, 0)
        ops.append({"q": q, "fn": fn, "r": reads, "w": writes, "cost": cost, "gat": gat, "late": late, "sem": sem, "inc": inc, "after": after})
        return len(ops) - 1

    def R(name, lo=0, hi=None, step=1, p1=128):
        t = T[name]
        if hi is None:
            hi = t.shape[1]
        return (t[0:p1, lo:hi] if step == 1 else t[0:p1, lo:hi:step], name, lo, hi, (hi - lo + step - 1) // step)

    def R4(name, e, rows=128):
        return (T[name][0:rows, :, e, :], name, 0, 512, 256)

    def IND(win, off):
        return (win[0].indirect(off[0]), win[1], win[2], win[3], 16 * off[4], off)

    def rd(*aps):
        out = []
        for a in aps:
            if isinstance(a, tuple):
                out.append(a)
                if len(a) == 6:
                    out.append(a[5])
        return out

    def val(a):
        return a[0] if isinstance(a, tuple) else a

    def price(out, a, rate=1.0, fast=True, more=0.0):
        if len(a) == 6:
            return (0.055, a[4])
        if fast and SCRATCH[out[1]][2] in (BF, U16) and SCRATCH[a[1]][2] in (BF, U16):
            rate = 0.5
        return (max(64, a[4] * rate) * CYC + more, 0)

    def copy(out, in_):
        add("V", lambda h: h.tensor_copy(out[0], in_[0]), rd(in_), [out], price(out, in_))

    def tt(out, a, b, op):
        one = a[1].startswith("ps") or b[1].startswith("ps")
        add("V", lambda h: h.tensor_tensor(out[0], a[0], b[0], op), rd(a, b), [out], price(out, a, 1.0 if one else 2.0, False))

    def ts(out, a, s1, op0, s2=None, op1=None):
        if op1 is None:
            add("V", lambda h: h.tensor_scalar(out[0], a[0], val(s1), None, op0), rd(a, s1), [out], price(out, a))
        else:
            add("V", lambda h: h.tensor_scalar(out[0], a[0], val(s1), val(s2), op0, op1), rd(a, s1, s2), [out], price(out, a))

    def memset(out, c):
        add("V", lambda h: h.memset(out[0], c), [], [out], price(out, out))

    def act(out, a, func=ACT.Identity, scale=None, bias=None, more=0.0):
        kw = {}
        if scale is not None:
            kw["scale"] = val(scale)
        if bias is not None:
            kw["bias"] = val(bias)
        add("S", lambda h: h.activation(out[0], a[0], func, **kw), rd(a, scale, bias), [out], price(out, a, 1.0, False, more))

    def either(on_v, v_call, s_call):
        v_call()
        s_call()
        s, v = ops.pop(), ops.pop()
        if on_v != (len(ops) in CFG["flip"]):
            s, v = v, s
        s["alt"] = v
        ops.append(s)

    def move(out, in_, on_v):
        either(on_v, lambda: copy(out, in_), lambda: act(out, in_))

    def affine(out, in_, scale, bias, on_v):
        either(on_v, lambda: ts(out, in_, scale, ALU.mult, bias, ALU.add), lambda: act(out, in_, scale=scale, bias=bias))

    def mms(calls):
        def fn(h):
            for o, l, x, a, b in calls:
                ins = h.matmul(o[0], l[0], x[0], a, b)
            return ins
        cost = sum(max(64, x[4]) * (4 if SCRATCH[x[1]][2] == F32 else 1) for o, l, x, a, b in calls) * CFG["pe"]
        add("P", fn, [c[1] for c in calls] + [c[2] for c in calls], [c[0] for c in calls], cost)

    def turn(out, sel, buf, lo, hi, start, stop):
        mms([(out, R(sel, 15 - q, 143 - q), R(buf, lo + q, hi, 16), start and q == 0, stop and q == 15) for q in range(16)])

    def iota(out, pattern, base, cm, flt=True):
        cost = 0.15 + out[4] * 2 * CYC
        if flt:
            add("G", lambda h: h.iota(out[0], pattern, base, cm, allow_small_or_imprecise_dtypes=True), [], [out], cost)
        else:
            add("G", lambda h: h.iota(out[0], pattern, base, cm), [], [out], cost)

    def select(out, in_, op, fill, pattern=((-1, 128),), base=0, cm=1):
        add("G", lambda h: h.affine_select(out[0], in_[0], [list(x) for x in pattern], op, fill, base, cm), [in_], [out], 0.19 + out[4] * 2 * CYC)

    def dma(q, out, in_, adding=False, late=None, after=()):
        s = "d%d" % ndma[0]
        ndma[0] += 1
        late = CFG["dma"] if late is None else late
        if adding:
            return add(q, lambda h: h.dma_start(val(out), val(in_), accum_op=ALU.add), rd(in_, out), rd(out), 1.0, late + 1.0, s, after=after)
        return add(q, lambda h: h.dma_start(val(out), val(in_)), rd(in_), rd(out), 0.06, late, s, after=after)

    here = topo.chip(core)
    dest = {d: T.cores[(r + d) % N] for d in range(1, N)}
    near = [d for d in dest if topo.chip(dest[d]) == here]
    mate = [d for d in dest if topo.mates(here, topo.chip(dest[d]))]
    plane = [d for d in dest if topo.same_plane(here, topo.chip(dest[d]))]
    both = [d for d in dest if d not in near + mate + plane]
    chunks = [both, [plane[0], mate[0]], [plane[1], mate[1]] + near]
    order = [d for ch in chunks for d in ch]
    far_engines = topo.engines(core, dest[both[0]])
    share = len(far_engines) // 2

    dma("S", R("pathi", 0, 512), T.path0[:, 0:512], late=1.9)
    dma("Y", R("pathi", 512, V), T.path0[:, 512:V], late=2.4)
    dma("Y", R("nbi"), T.nb[:], late=2.9)
    for k in range(8):
        dma("YS"[k & 1], (T.X[:, k], "X", 64 * k, 64 * k + 64, 64), T.lk[k], late=4.0)
    for k in range(8):
        last_load = dma("Y", (T.O[0:16, k], "O", 64 * k, 64 * k + 64, 64), T.org[k], late=4.5)
    for k, d in enumerate(order):
        dma("Y", R("shi", 16 * k, 16 * k + 16), T.shown[:, 16 * d - 16:16 * d], after=[last_load])
    dma("Y", R("ati"), T.at0[:], after=[last_load])
    dma("Y", R("TL"), T.toll[:], after=[last_load])

    iota(R("kci", 0, 1), [[0, 1]], 0, 1, flt=False)
    ops[-1]["first"] = True
    iota(R("NF0"), [[2, 512]], r * V + 1, 0)
    ops[-1]["first"] = True
    memset(R("ONE"), 1.0)
    memset(R("SV"), 1.0)
    select(R("IDb"), R("ONE", 0, 128), ALU.is_equal, 0.0)
    select(R("IDf"), R("SV"), ALU.is_equal, 0.0)
    for k in range(4):
        select(R("SHF", 128 * k, 128 * k + 128), R("SV"), ALU.is_equal, 0.0, ((-16, 8), (256, 2), (-2, 8)), -256 * (k & 1) - (k >> 1))
    select(R("RST"), R("ONE", 0, 112), ALU.not_equal, 0.0, ((0, 7), (1, 16)), 0, 0)
    for n in ("DP", "DN"):
        iota(R(n), [[0, T[n].shape[1]]], 0, 0)
    iota(R("RG"), [[1, 8], [0, 16]], 0, 0)
    iota(R("RQ"), [[0, 8], [1, 16]], 0, 0)
    iota(R("DN8"), [[1, 2], [32, 32]], 0, 0)
    iota(R("slot"), [[16, 112]], 0, 0)

    GC, QC, Q0, Q14, Q15, KC, QN, Q2, WE, WM, W1, W2, W3, WS, WC, WN = [R("col", j, j + 1) for j in range(16)]
    for n in ("MEQ", "MM", "MNE", "ZT", "DP0", "MPK"):
        memset(R(n), 0.0)
    ts(R("gqi", 0, 1), R("kci", 0, 1), 4, ALU.arith_shift_right)
    ts(R("gqi", 1, 2), R("kci", 0, 1), 15, ALU.bitwise_and)
    copy(R("col", 0, 2), R("gqi", 0, 2))
    ts(Q0, QC, 0.0, ALU.is_equal)
    ts(Q14, QC, 14.0, ALU.is_equal)
    ts(Q15, QC, 15.0, ALU.is_equal)
    ts(KC, GC, -4096.0, ALU.mult, 4096.0 * 7, ALU.add)
    ts(WE, QC, 15.0, ALU.is_lt, -BIG, ALU.mult)
    ts(WM, QC, 15.0, ALU.is_equal, 32768.0, ALU.mult)
    act(W1, Q15, scale=-2.0, bias=1.0)
    act(W2, Q0, scale=-257.0, bias=1.0)
    act(W3, Q15, scale=255.0, bias=W2)
    act(WS, Q14, scale=-1.0, bias=Q15)
    ts(WC, Q15, 1e18, ALU.mult, 1e17, ALU.mult)
    act(WN, Q15, scale=-1.0)
    ts(QN, QC, 0.0, ALU.not_equal, 1e18, ALU.mult)
    ts(QN, QN, 1e17, ALU.mult)
    act(Q2, QC, scale=2.0)

    def spread(out, w):
        ts(out, R("RG", 0, 128, 16), GC, ALU.is_equal, w, ALU.mult)

    spread(R("MEQ", 15, 143, 16), WE)
    spread(R("MM", 15, 143, 16), WM)
    spread(R("MNE", 15, 143, 16), -1.0)
    spread(R("MPK", 15, 143, 16), Q0)
    ts(R("ZT", 0, 1), Q15, -241.0, ALU.mult)
    ts(R("ZT", 1, 2), Q14, 240.0, ALU.mult)
    ts(R("ZT", 2, 3), Q15, 16.0, ALU.mult)
    ts(R("BOS"), R("RG"), GC, ALU.is_equal, -8192.0, ALU.mult)
    for n, c in (("D1", W1), ("D2", -255.0), ("D15", WN), ("I19", float(1 << 19)), ("N23", -float(1 << 23)), ("NEG", -BIG), ("I192", 192.0 * (1 << 23)),
                 ("DK", KC), ("I4", 4.0), ("I256", -256.0)):
        affine(R(n), R("IDb"), c, 0.0, False)
    spread(R("D2", 15, 128, 16), W3)
    for n in ("SHT", "SHU"):
        select(R(n), R("ONE", 0, 128), ALU.is_equal, 0.0, base=1)
        spread(R(n, 0, 128, 16), WC)
    spread(R("SHT", 15, 128, 16), WS)
    select(R("TMS"), R("BOS"), ALU.is_gt, 0.0)
    select(R("TMS"), R("TMS"), ALU.not_equal, -float(1 << 21))
    move(R("B0", V, V + 16), R("ZT"), True)
    move(R("B1", 0, 16), R("ZT"), False)
    for t in (1, 2, 3):
        move(R("B%d" % t, PRE[t] + W, PRE[t] + W + 16), R("ZT"), False)

    act(R("NM0"), R("NF0"), ACT.Exp, STEP, BASE, 1.3)
    ops[-1]["first"] = True
    for hf in range(2):
        lo, hi = 512 * hf, 512 * hf + 512
        copy(R("PF", lo, hi), R("pathi", lo, hi))
        act(R("EN", lo, hi), R("PF", lo, hi), ACT.Exp, STEP, BASE)
        ts(R("FLG", lo, hi), R("EN", lo, hi), 255.0, ALU.is_equal)
        mms([(R("ps%d" % hf), R("D1"), R("EN", lo, hi), True, False)])
        mms([(R("ps%d" % hf), R("D2"), R("FLG", lo, hi), False, True)])
        move(R("B0", lo, hi), R("ps%d" % hf), hf == 1)
    iota(R("NF1"), [[2, 512]], r * V + 2, 0)
    act(R("NM1"), R("NF1"), ACT.Exp, STEP, BASE)
    for pi in range(2):
        act(R("ps%d" % (6 + pi)), R("NM%d" % pi))
        affine(R("TT%d" % pi), R("NM%d" % pi), Q0, QN, True)

    def shuffle(out, pi, e, first):
        return [(out, R("SHF", 128 * (2 * pi + hh), 128 * (2 * pi + hh) + 128), R("nbf", 2 * e + hh, 512, 4), first and hh == 0, hh == 1) for hh in range(2)]

    copy(R("nbf"), R("nbi"))
    for pi in range(2):
        b = "ps%d" % (2 + 2 * pi)
        mms(shuffle(R(b, 0, 128), pi, 0, True) + shuffle(R(b, 128, 256), pi, 1, True))
        for e in range(2):
            ts(R("L0", 256 * pi + e, 256 * pi + 256, 2), R(b, 128 * e, 128 * e + 128), float(V), ALU.min)
        for e in range(2):
            copy(R("L", 256 * pi + e, 256 * pi + 256, 2), R(b, 128 * e, 128 * e + 128))

    for e in range(2):
        copy(R("Xb", 256 * e, 256 * e + 256), R4("X", e))
        copy(R("Ob", 256 * e, 256 * e + 256, p1=16), R4("O", e, 16))
    affine(R("DNb"), R("Xb"), 1.0 / 16, 192.0 - 15.0 / 32, False)
    ts(R("R16", p1=16), R("RQ", p1=16), R("col", 1, 2, p1=16), ALU.is_equal, -256.0, ALU.mult)

    def link_tables(pi):
        for e in range(2):
            o = R("ps3", 128 * e, 128 * e + 128)
            ob = R("Ob", 256 * e + pi, 256 * e + 256, 2, p1=16)
            mms([(o, R("Xb", 256 * e + pi, 256 * e + 256, 2), R("IDb"), True, False), (o, ob, R("R16", p1=16), False, True),
                 (R("ps3", 256 + 16 * e, 272 + 16 * e), ob, R("IDb", 0, 16, p1=16), True, True)])
        for e in range(2):
            o = R("ps5", 128 * e, 128 * e + 128)
            mms([(o, R("Xb", 256 * e + pi, 256 * e + 256, 2), R("I19"), True, False), (o, R("DNb", 256 * e + pi, 256 * e + 256, 2), R("N23"), False, False),
                 (o, R("ONE", 0, 128), R("I192"), False, False), (o, R("ONE", 0, 128), R("DK"), False, False)] + shuffle(o, pi, e, False))
        for e in range(2):
            move(R("LK", 256 * pi + e, 256 * pi + 256, 2), R("ps3", 128 * e, 128 * e + 128), False)
            move(R("CST", 256 * pi + e, 256 * pi + 256, 2), R("ps5", 128 * e, 128 * e + 128), False)
            src = R("ps3", 256 + 16 * e, 272 + 16 * e)
            if pi == 0:
                act(R("DP0", e, 32, 2), src, bias=float(V + 1))
            act(R("DP", 64 * pi + e, 64 * pi + 32, 2), src, bias=float(W + 1))
        for t in range(RO):
            ts(R("DT%d" % t, 256 * pi, 256 * pi + 256), R("LK", 256 * pi, 256 * pi + 256), 16.0 * (t + 1), ALU.is_lt)

    link_tables(0)
    link_tables(1)
    copy(R("shu"), R("shi"))
    memset(R("C191"), 191.0 / 16)
    ts(R("SA0"), R("shi"), float(PRE[1]), ALU.add)
    for pi in range(2):
        ts(R("DN", 128 * pi, 128 * pi + 32), R("DN8", 32 * pi, 32 * pi + 32), Q2, ALU.add)
    ts(R("DN8"), R("DN8"), Q2, ALU.add, 8192.0, ALU.add)
    act(R("SA1"), R("SA0"), bias=float(GH - PRE[1]))
    act(R("slot"), R("slot"), bias=QC)
    copy(R("atu"), R("ati"))
    for k in range(4):
        iota(R("TP", 704 * k, 704 * k + 704), [[1024, 704]], 1024 * 704 * k, 0)

    def window(t):
        return R("B%d" % t, PRE[t], PRE[t] + (V if t == 0 else W) + 16)

    def neighbours(t, pi, c, k, on_v, whole):
        for i, n in ((2 * c, 2),) if whole else ((2 * c, 1), (2 * c + 1, 1)):
            src = IND(window(t), R("L0" if t == 0 else "L", 256 * pi + 32 * i, 256 * pi + 32 * (i + n)))
            move(R("GA%d" % k, 512 * i, 512 * (i + n)), src, on_v and i == 2 * c)
        for i in (2 * c, 2 * c + 1):
            tt(R("EQ%d" % k, 512 * i, 512 * i + 512), R("GA%d" % k, 512 * i, 512 * i + 512), R("ps%d" % (6 + pi)), ALU.is_equal)

    def scores(t, pi, i0, i1, k, o):
        lo, hi = 256 * pi + 32 * i0, 256 * pi + 32 * i1
        late = (t, pi) == (0, 0) and i1 < 6
        if not late:
            mms([(o, R("IDf"), R("CST", lo, hi), True, False), (o, R("NEG"), R("DT%d" % t, lo, hi), False, False)])
        turn(o, "MM", "GA%d" % k, 512 * i0, 512 * i1, late, False)
        turn(o, "MEQ", "EQ%d" % k, 512 * i0, 512 * i1, False, not late)
        if late:
            mms([(o, R("IDf"), R("CST", lo, hi), False, False), (o, R("NEG"), R("DT%d" % t, lo, hi), False, True)])

    def nh_list(t, pi):
        return R("NH", 64 * t + 32 * pi, 64 * t + 32 * pi + 32)

    def advertisers(t):
        pi = t & 1
        prev = R("DP0" if t == 0 else "DP", 64 * pi, 64 * pi + 64)
        for c in range(4):
            neighbours(t, pi, c, 0, c == 0, c in CFG["wc"])
            o = R("ps%d" % (c & 1), 0, 64)
            scores(t, pi, 2 * c, 2 * c + 2, 0, o)
            tt(R("RUN", 64 * c, 64 * c + 64), o, prev, ALU.max)
            prev = R("RUN", 64 * c, 64 * c + 64)
        tt(R("RI", 0, 32), R("RUN", 192, 224), R("RUN", 224, 256), ALU.max)
        ts(R("RA", 0, 32), R("RI", 0, 32), 4095, ALU.bitwise_and)
        copy(R("PL", 32 * t, 32 * t + 32), R("RA", 0, 32))
        if t == RO - 1:
            tt(R("NI", 0, 32), R("RI", 0, 32), R("DN8", 32 * pi, 32 * pi + 32), ALU.max)
            ts(R("NA", 0, 32), R("NI", 0, 32), 4095, ALU.bitwise_and)
            copy(nh_list(t, pi), R("NA", 0, 32))
        else:
            tt(R("NI", 32 * pi, 32 * pi + 32), R("RI", 0, 32), R("DN8", 32 * pi, 32 * pi + 32), ALU.max)

    def others(t):
        pi, k = 1 - (t & 1), 1 + (t & 1)
        for c in range(4):
            neighbours(t, pi, c, k, c == 0, c in CFG["wn"])
            scores(t, pi, 2 * c, 2 * c + 2, k, R("ps2", 64 * c, 64 * c + 64))
        tt(R("RUN2", 0, 128), R("ps2", 0, 128), R("DN", 128 * pi, 128 * pi + 128), ALU.max)
        tt(R("RUN2", 128, 256), R("ps2", 128, 256), R("RUN2", 0, 128), ALU.max)
        tt(R("RUN2", 256, 320), R("RUN2", 128, 192), R("RUN2", 192, 256), ALU.max)
        if t == RO - 1:
            tt(R("RI", 32, 64), R("RUN2", 256, 288), R("RUN2", 288, 320), ALU.max)
            ts(R("RA", 32, 64), R("RI", 32, 64), 4095, ALU.bitwise_and)
            copy(nh_list(t, pi), R("RA", 32, 64))
        else:
            tt(R("NI", 32 * pi, 32 * pi + 32), R("RUN2", 256, 288), R("RUN2", 288, 320), ALU.max)
            ts(R("NA"), R("NI"), 4095, ALU.bitwise_and)
            copy(R("NH", 64 * t, 64 * t + 64), R("NA"))

    def advertise(t):
        pi = t & 1
        for hf in range(2):
            pg, tt_ = R("PG", 256 * hf, 256 * hf + 256), R("TT%d" % pi, 256 * hf, 256 * hf + 256)
            move(pg, IND(window(t), R("PL", 32 * t + 16 * hf, 32 * t + 16 * hf + 16)), hf == 1)
            if t < RO - 1:
                o = R("ps%d" % (3 * hf), 0, 256)
                mms([(o, R("D15"), R("ONE"), True, False)])
                mms([(o, R("SHT"), pg, False, True)])
                lo = PRE[t + 1] + 512 * hf
                tt(R("B%d" % (t + 1), lo + pi, lo + 512, 2), o, tt_, ALU.min)
        if t >= RO - 2:
            for hf in range(2):
                lo, hi = 256 * hf, 256 * hf + 256
                o = R("ps%d" % (3 if t < RO - 1 else 3 * hf), lo, hi)
                mms([(o, R("SHU"), R("PG", lo, hi), True, True)])
                tt(R("YE", lo, hi), o, R("TT%d" % pi, lo, hi), ALU.min)
                act(R("YL", lo, hi), R("YE", lo, hi), ACT.Ln, math.exp(-(BASE + STEP * MID)), math.exp(-43.0), 1.5 if (t, hf) == (RO - 2, 0) else 0.0)
                affine(R("YR", lo, hi), R("YL", lo, hi), 1.0 / STEP, RND + MID, False)
                yp = R("YP", 2 * lo + pi, 2 * hi, 2)
                either(False, lambda: ts(yp, R("YR", lo, hi), RND, ALU.max, RND, ALU.subtract), lambda: act(yp, R("YR", lo, hi), ACT.Relu, bias=-RND))
                if t == RO - 1:
                    dma("Y", T.ypath[:, 2 * lo:2 * hi], R("YP", 2 * lo, 2 * hi))

    def carry(t, pi):
        select(R("B%d" % (t + 1), PRE[t + 1] + pi, PRE[t + 1] + V, 2), R("B%d" % t, PRE[t] + pi, PRE[t] + V, 2), ALU.is_ge, 0.0, ((0, 512),), 0, 0)

    def masks(ch):
        out, k = {}, 0
        for d in ch:
            if d in near:
                es = [e for e in topo.engines(core, dest[d]) if e not in far_engines][:share]
            else:
                es = far_engines[k * share:(k + 1) * share]
                k += 1
            out[d] = sum(1 << e for e in es)
        return out

    def crossing(t):
        b, last = "B%d" % (t + 1), "SND" if t == 2 else "B%d" % (t + 2)
        sends = []
        for j, ch in enumerate(chunks):
            m0, m1 = 16 * order.index(ch[0]), 16 * order.index(ch[-1]) + 16
            mid = ((m0 + m1) // 4) * 2
            for n0, n1 in ((m0, m1),) if t > 0 else ((m0, mid), (mid, m1)):
                src = IND(R(b, PRE[t + 1], PRE[t + 1] + V), R("shu", n0, n1))
                out = R("NE", 16 * n0, 16 * n1)
                if t > 0:
                    tt(out, src, R(b, 16 * n0, 16 * n1), ALU.not_equal)
                else:
                    either(n0 == m0, lambda: ts(out, src, 0.0, ALU.not_equal), lambda: act(out, src, ACT.Sign))
            ps = R("ps%d" % (0 if j & 1 else 4), 0, m1 - m0)
            turn(ps, "MNE" if t > 0 else "MEQ", "NE", 16 * m0, 16 * m1, True, True)
            o, a, c = R("SC", m0, m1), R("RST", m0, m1), R("CH", m0, m1)
            either(False, lambda: ts(c, ps, 0.0, ALU.is_lt, -1.0, ALU.mult), lambda: act(c, ps, ACT.Sign))
            add("V", lambda h, o=o, a=a, c=c: h.tensor_tensor_scan(o[0], a[0], c[0], 0.0, ALU.mult, ALU.subtract), [a, c], [o], 0.055)
            ps = R("ps%d" % (1 if j & 1 else 5), 0, m1 - m0)
            mms([(ps, R("BOS"), R("C191", m0, m1), True, False)])
            mms([(ps, R("TMS"), c, False, False)])
            mms([(ps, R("BOS"), o, False, True)])
            tt(R("M1", m0, m1), ps, R("SA0" if t == 0 else "SA1", m0, m1), ALU.min)
            if t == 0:
                copy(R("XI", m0, m1), R("M1", m0, m1))
            else:
                tt(R("M2", m0, m1), R("M1", m0, m1), R("slot", m0, m1), ALU.max)
                copy(R("XI", m0, m1), R("M2", m0, m1))
            win = R(b, 0, PRE[t + 1] + V)
            move(R(last, 16 * m0, 16 * mid), IND(win, R("XI", m0, mid)), False)
            move(R(last, 16 * mid, 16 * m1), IND(win, R("XI", mid, m1)), True)
            mk = masks(ch)
            trs = []
            for d in ch:
                rid, pid, se = topo.addr(dest[d])
                lo, at = PRE[t + 1] + V + G * (d - 1), G * order.index(d)
                trs.append(RemoteDMATransfer(dst_ids=[DstId(rid=rid, pnc=pid)], dma_engine_mask=mk[d], remote_sem=T.sem["arr%d" % t],
                                             src=T[last][:, at:at + G], dst=T[b][:, lo:lo + G]))
            n = add("G", lambda h, trs=trs: h.remote_dma_fused(trs, local_sem=T.sem.sent), [R(last, 16 * m0, 16 * m1)], [],
                    0.6, 0.0, "sent", share * len(trs))
            sends.append(add("X", None, [], [], CFG["blk"] * len([d for d in ch if d not in near]), CFG["fix"], None, 0, [n]))
        landed = [add("X", None, [], [R(b, PRE[t + 1] + V, PRE[t + 1] + W)], 0.0, 0.0, "arr%d" % t, share * (N - 1), sends)]
        if t == 0:
            dma("G", R("TP", 0, V), T.toll[:, 0:V], True, after=landed)
            dma("G", R("TP", V, W), T.toll[:, V:W], True, after=landed)
            dma("Y", R("U2", V, W), R("TP", V, W))
        if t == 1:
            dma("G", R("U2", V, W), T.toll[:, V:W], True, after=landed)
            dma("Y", R("H", V, W), T.toll[:, V:W], after=landed)

    carry(0, 1)
    for t in range(RO):
        advertisers(t)
        advertise(t)
        if t < RO - 1:
            crossing(t)
        if t < RO - 2:
            carry(t + 1, t & 1)
        others(t)
        if t == 0:
            for k in range(4):
                lo = 448 * k
                affine(R("FL", lo, lo + 448), R("TL", V + lo, V + lo + 448), 1.0 / 64, 192.0 - 63.0 / 128, True)
                mms([(R("ps2", 0, 448), R("I4"), R("TL", V + lo, V + lo + 448), True, False), (R("ps2", 0, 448), R("I256"), R("FL", lo, lo + 448), False, True)])
                affine(R("FW", V + lo, V + lo + 448), R("ps2", 0, 448), 1.0, 49152.0, False)
        if t == 2:
            for pi in range(2):
                tt(R("U2", pi, V, 2), IND(R("TP"), nh_list(2, pi)), R("TL", pi, V, 2), ALU.add)
            for pi in range(2):
                tt(R("U1", pi, V, 2), IND(R("U2"), nh_list(1, pi)), R("TL", pi, V, 2), ALU.add)
            for pi in range(2):
                move(R("T0", pi, V, 2), IND(R("U1"), nh_list(0, pi)), False)
            turn(R("ps4", 0, 64), "MPK", "T0", 0, V, True, True)
            copy(R("QI"), R("ps4", 0, 64))
            ts(R("QA"), R("QI"), 10, ALU.arith_shift_right)
            copy(R("Q"), R("QA"))

    move(R("H", 1, V, 2), IND(R("TL"), nh_list(3, 1)), False)
    for hf in range(2):
        move(R("H", 512 * hf, 512 * hf + 512, 2), IND(R("TL"), R("NH", 192 + 16 * hf, 208 + 16 * hf)), hf == 1)
    for hf in range(2):
        lo, hi = 512 * hf, 512 * hf + 512
        tt(R("ZI", lo, hi), IND(R("H"), R("Q", 32 * hf, 32 * hf + 32)), R("T0", lo, hi), ALU.add)
        ts(R("ZA", lo, hi), R("ZI", lo, hi), 255, ALU.bitwise_and)
        copy(R("FW", lo, hi), R("ZA", lo, hi))
    for k in range(4):
        lo = 512 * k
        move(R("YS", lo, lo + 512), IND(R("FW"), R("atu", 32 * k, 32 * k + 32)), k & 1 == 0)
        dma("Y", T.ysum[:, lo:lo + 512], R("YS", lo, lo + 512))
    emit(ops, g, T)
